import numpy as np
import ml_dtypes


def mxq(x, axis, fmt="e4m3"):
    dtype, down = {"e4m3": (ml_dtypes.float8_e4m3fn, 7), "e5m2": (ml_dtypes.float8_e5m2, 14)}[fmt]
    v = np.moveaxis(np.asarray(x, np.float32).astype(ml_dtypes.bfloat16).astype(np.float64), axis, -1)
    blocks = v.reshape(v.shape[:-1] + (-1, 32))
    amax = np.abs(blocks).max(-1, keepdims=True)
    byte = np.maximum(np.where(amax > 0, np.frexp(amax)[1] - 1 + 127, 0) - down, 1)
    scale = np.exp2(byte - 127.0)
    codes = (blocks / scale).astype(np.float32).astype(dtype).astype(np.float64)
    return np.moveaxis((codes * scale).reshape(v.shape), -1, axis)


WIDE = False


def mx_kscale(k):
    if not WIDE:
        return np.ones(k)
    levels = np.array([10, -10, 5, -5, 0])
    if k % 512:
        return np.exp2(np.random.permutation(np.resize(levels, k // 32))).repeat(32)
    a = np.empty((k // 512, 16))
    for p in range(k // 512):
        a[p, :8] = np.random.permutation(np.resize(levels, 8))
        for g in range(8):
            far = levels[np.abs(levels - a[p, g]) >= 10]
            a[p, g + 8] = far[np.random.randint(len(far))]
    return np.exp2(a.ravel()).repeat(32)


def f64(x):
    return np.asarray(x).astype(np.float64)


def striped(idx):
    return np.tile(idx.reshape(-1, 16).T, (8, 1)).astype(np.uint16)


def unstriped(offs):
    return offs[:16].T.reshape(-1).astype(np.int64)


E2M1 = np.array([0.0, 0.5, 1.0, 1.5, 2.0, 3.0, 4.0, 6.0, -0.0, -0.5, -1.0, -1.5, -2.0, -3.0, -4.0, -6.0])


def pack_weight(w, fmt):
    k, n = w.shape
    w = f64(np.asarray(w, np.float32).astype(ml_dtypes.bfloat16)).reshape(k // 32, 32, n)
    amax = np.abs(w).max(1)
    if fmt == "e4m3":
        byte = np.frexp(amax)[1] - 1 + 127 - 7
    else:
        mant, ex = np.frexp(amax / 6.0)
        byte = np.where(mant > 0.5, ex, ex - 1) + 127
    byte = np.clip(np.where(amax > 0, byte, 1), 1, 254)
    scaled = (w * np.exp2(127.0 - byte)[:, None, :]).reshape(k, n).astype(np.float32)
    by_word = np.ascontiguousarray(scaled.reshape(k // 512, 128, 4, n).transpose(0, 1, 3, 2))
    if fmt == "e4m3":
        words = by_word.astype(ml_dtypes.float8_e4m3fn).view(np.uint8)
    else:
        c = by_word.astype(ml_dtypes.float4_e2m1fn).view(np.uint8) & 0xF
        words = (c[..., 0::2] | (c[..., 1::2] << 4)).reshape(k // 512, 128, 2 * n)
    return np.ascontiguousarray(words), np.ascontiguousarray(byte.astype(np.uint8).reshape(k // 512, 16, n))


def unpack_weight(words, scales, fmt):
    g, _, n = scales.shape
    words = np.ascontiguousarray(words).reshape(g, 128, n, -1)
    if fmt == "e4m3":
        vals = words.view(ml_dtypes.float8_e4m3fn).astype(np.float64)
    else:
        nib = np.empty((g, 128, n, 4), np.uint8)
        nib[..., 0::2] = words & 0xF
        nib[..., 1::2] = words >> 4
        vals = E2M1[nib]
    vals = vals * np.repeat(np.exp2(scales.astype(np.float64) - 127.0), 8, axis=1)[..., None]
    return vals.transpose(0, 1, 3, 2).reshape(g * 512, n)


def d_relu(v):
    return (v > 0).astype(np.float64)


K, T, E, C, H, N, TOP = 256, 512, 16, 128, 512, 512, 4


def by_expert(wq, xq):
    return np.concatenate([wq[e].T @ xq[:, e * C:(e + 1) * C] for e in range(E)], axis=1)


def setup_inputs():
    n = np.random.standard_normal
    v = mx_kscale(N)
    u = mx_kscale(H)
    deal = np.repeat(np.arange(E), C).reshape(TOP, T)[:, np.random.permutation(T)]
    deal = np.take_along_axis(deal, np.argsort(np.random.rand(TOP, T), axis=0), axis=0)
    for _ in range(8):
        s_, t_ = np.random.permutation(T).reshape(2, -1); r = np.random.randint(TOP, size=T // 2); x, y = deal[r, s_].copy(), deal[r, t_].copy()
        ok = ~((deal[:, s_] == y).any(0) | (deal[:, t_] == x).any(0)); deal[r[ok], s_[ok]] = y[ok]; deal[r[ok], t_[ok]] = x[ok]
    order = np.lexsort((np.random.rand(TOP * T), deal.reshape(-1)))
    slot_token = order % T; pos = np.empty(TOP * T, np.int64); pos[order] = np.arange(TOP * T); pos = pos.reshape(TOP, T)
    g = np.random.uniform(0.5, 1.5, (TOP, T)); g = g / g.sum(0)
    dy = pack_weight(n((N, T)) * v[:, None], "e4m3")
    w2t = [pack_weight(m, "e2m1") for m in n((E, N, H)) / np.sqrt(N) / v[None, :, None] * u]
    return {
        "dy_words": dy[0],
        "dy_scales": dy[1],
        "w2t_words": np.stack([m[0] for m in w2t]),
        "w2t_scales": np.stack([m[1] for m in w2t]),
        "w1t": (n((H, K)) / np.sqrt(H) / u[:, None]).astype(np.float32),
        "a": (n((H, T))).astype(np.float32),
        "gate": np.stack([np.tile(r, (128, 1)) for r in g]).astype(np.float32),
        "offs": striped(slot_token),
        "pos1": striped(pos[0]),
        "pos2": striped(pos[1]),
        "pos3": striped(pos[2]),
        "pos4": striped(pos[3]),
    }


def reference(dy_words, dy_scales, w2t_words, w2t_scales, w1t, a, gate, offs, pos1, pos2, pos3, pos4):
    w2t = np.stack([unpack_weight(w2t_words[e], w2t_scales[e], "e2m1") for e in range(E)])
    w1tq = mxq(f64(w1t), 0, "e4m3")
    idx = unstriped(offs)
    gq = unpack_weight(dy_words, dy_scales, "e4m3")[:, idx]
    y = by_expert(w2t, gq)
    dh = sum(f64(gate[r, :1]) * y[:, unstriped(p)] for r, p in enumerate((pos1, pos2, pos3, pos4)))
    return w1tq.T @ mxq(dh * d_relu(f64(a)), 0, "e4m3")

@@ -1,0 +1,204 @@
+from contextlib import ExitStack
+
+import concourse.mybir as mybir
+from concourse.masks import make_identity
+
+K, T, E, C, H, N, TOP = 256, 512, 16, 128, 512, 512, 4
+FLOPS = 2 * N * H * E * C + 2 * H * K * T
+
+F32 = mybir.dt.float32
+BF16 = mybir.dt.bfloat16
+I32 = mybir.dt.int32
+U32 = mybir.dt.uint32
+U16 = mybir.dt.uint16
+U8 = mybir.dt.uint8
+FP8X4 = mybir.dt.float8_e4m3fn_x4
+FP4X4 = mybir.dt.float4_e2m1fn_x4
+ALU = mybir.AluOpType
+
+P = 128
+S = E * C
+HT = H // P
+TT = T // P
+WINDOW = 2 * T
+WORD_PIECES = ((0, 6), (6, 12), (12, 16))
+BYTE_PIECES = ((0, 6), (6, 12), (12, 15), (15, 16))
+FIRST_GROUPS = ((0, 4), (4, 8), (8, 12), (12, 15), (15, 16))
+GROUPS = ((0, 4), (4, 8), (8, 12), (12, 16))
+LAST_SPANS = ((0, 3), (3, 4))
+OUT_SPANS = ((0, 2), (2, 3), (3, 4))
+
+
+def tile_moe_sub_relu_kernel(
+    tc, dy_words, dy_scales, w2t_words, w2t_scales, w1t, a, gate, offs, pos1, pos2, pos3, pos4, out
+):
+    nc = tc.nc
+    with ExitStack() as ctx:
+        keep = ctx.enter_context(tc.tile_pool(name="keep", bufs=1))
+        ring = ctx.enter_context(tc.tile_pool(name="ring", bufs=6))
+        work = ctx.enter_context(tc.psum_pool(name="work", bufs=6))
+        sums = ctx.enter_context(tc.psum_pool(name="sums", bufs=2))
+
+        offs_sb = keep.tile([P, S // 16], U16, name="offs_sb")
+        pos_sb = [keep.tile([P, T // 16], U16, name=f"pos_sb{r}") for r in range(TOP)]
+        dy_w = keep.tile([P, WINDOW], I32, name="dy_w", align_bytes=64)
+        dy_s = keep.tile([P, WINDOW], U8, name="dy_s", align_bytes=64)
+        slot_w = keep.tile([P, S], U32, name="slot_w", align_bytes=64)
+        slot_s = keep.tile([P, S], U8, name="slot_s", align_bytes=64)
+        w2_w = keep.tile([P, E, 2 * H], U8, name="w2_w", align_bytes=64)
+        w2_s = keep.tile([P, E, H], U8, name="w2_s", align_bytes=64)
+        gate_sb = keep.tile([P, TOP, T], F32, name="gate_sb")
+        a_sb = keep.tile([P, HT, T], F32, name="a_sb")
+        a_t = keep.tile([P, HT, TT, P], F32, name="a_t")
+        w1_raw = keep.tile([P, 4, K], F32, name="w1_raw")
+        w1_bf = keep.tile([P, K, 4], BF16, name="w1_bf", align_bytes=64)
+        w1_w = keep.tile([P, K], U32, name="w1_w", align_bytes=64)
+        w1_s = keep.tile([P, K], U8, name="w1_s", align_bytes=64)
+        y = [keep.tile([P, S], F32, name=f"y{c}") for c in range(HT)]
+        da_t = keep.tile([P, TT, H], BF16, name="da_t", align_bytes=64)
+        da_bf = keep.tile([P, T, 4], BF16, name="da_bf", align_bytes=64)
+        da_w = keep.tile([P, T], U32, name="da_w", align_bytes=64)
+        da_s = keep.tile([P, T], U8, name="da_s", align_bytes=64)
+        res = keep.tile([P, K // P, T], F32, name="res")
+        ident = keep.tile([P, P], F32, name="ident")
+
+        nc.vector.memset(dy_s[:].bitcast(I32), 0)
+        nc.vector.memset(w2_s[:].rearrange("p e i -> p (e i)").bitcast(I32), 0)
+        nc.vector.memset(dy_w[:, T:], 0)
+        make_identity(nc, ident[:])
+
+        nc.sync.dma_start(offs_sb[:], offs)
+        nc.sync.dma_start(dy_w[:, :T], dy_words[0].rearrange("p t d -> p (t d)").bitcast(I32))
+        for r in range(4):
+            nc.sync.dma_start(dy_s[r:P:32, :T].bitcast(I32), dy_scales[0, r:16:4, :].bitcast(I32))
+        for r in range(4):
+            nc.sync.dma_start(
+                w2_s[r:P:32, :, :].bitcast(I32),
+                w2t_scales[:, 0, r:16:4, :].rearrange("e q i -> q e i").bitcast(I32),
+            )
+        for e0, e1 in GROUPS:
+            nc.sync.dma_start(
+                w2_w[:, e0:e1, :].bitcast(I32),
+                w2t_words[e0:e1, 0].rearrange("e p b -> p e b").bitcast(I32),
+            )
+        for r, pos in enumerate((pos1, pos2, pos3, pos4)):
+            nc.sync.dma_start(pos_sb[r][:], pos)
+            nc.sync.dma_start(gate_sb[:, r, :], gate[r])
+        nc.sync.dma_start(a_sb[:], a.rearrange("(c p) t -> p c t", p=P))
+        nc.sync.dma_start(w1_raw[:], w1t.rearrange("(p d) k -> p d k", d=4))
+
+        for e0, e1 in WORD_PIECES:
+            nc.vector.tensor_copy(
+                slot_w[:, e0 * C : e1 * C],
+                dy_w[:].bitcast(U32).indirect(offs_sb[:, e0 * C // 16 : e1 * C // 16]),
+            )
+        for e0, e1 in BYTE_PIECES:
+            nc.vector.tensor_copy(
+                slot_s[:, e0 * C : e1 * C],
+                dy_s[:].indirect(offs_sb[:, e0 * C // 16 : e1 * C // 16]),
+            )
+
+        def expert_products(c, groups):
+            for e0, e1 in groups:
+                bank = work.tile([P, 4 * C], F32, name="bank")
+                for e in range(e0, e1):
+                    nc.tensor.matmul_mx(
+                        out=bank[:, (e - e0) * C : (e - e0 + 1) * C],
+                        lhsT=w2_w[:, e, 2 * P * c : 2 * P * (c + 1)].bitcast(FP4X4),
+                        lhsT_scale=w2_s[:, e, P * c : P * (c + 1)],
+                        rhs=slot_w[:, e * C : (e + 1) * C].bitcast(FP8X4),
+                        rhs_scale=slot_s[:, e * C : (e + 1) * C],
+                        start=True,
+                        stop=True,
+                    )
+                if e1 - e0 == 1:
+                    nc.vector.tensor_copy(y[c][:, e0 * C : e1 * C], bank[:, :C])
+                else:
+                    nc.scalar.copy(y[c][:, e0 * C : e1 * C], bank[:, : (e1 - e0) * C])
+
+        def turn_a(c):
+            bank = work.tile([P, 4 * C], F32, name="bank")
+            for j in range(TT):
+                nc.tensor.transpose(bank[:, j * P : (j + 1) * P], a_sb[:, c, j * P : (j + 1) * P], ident[:])
+            nc.scalar.copy(a_t[:, c].rearrange("p j i -> p (j i)"), bank[:])
+
+        def combine(c, j0, j1):
+            acc = sums.tile([P, T], F32, name="acc")
+            for r in range(TOP):
+                prod = ring.tile([P, T], F32, name="prod")
+                nc.vector.tensor_tensor(
+                    prod[:, : (j1 - j0) * P],
+                    y[c][:].indirect(pos_sb[r][:, j0 * P // 16 : j1 * P // 16]),
+                    gate_sb[:, r, j0 * P : j1 * P],
+                    ALU.mult,
+                )
+                for j in range(j1 - j0):
+                    nc.tensor.matmul(
+                        acc[:, j * P : (j + 1) * P],
+                        prod[:, j * P : (j + 1) * P],
+                        ident[:],
+                        start=(r == 0 and j == 0),
+                        stop=(r == TOP - 1 and j == j1 - j0 - 1),
+                        is_transpose=True,
+                    )
+            return acc
+
+        def mask(c, j0, j1, acc):
+            nc.vector.scalar_tensor_tensor(
+                out=da_t[:, j0:j1, c * P : (c + 1) * P],
+                in0=a_t[:, c, j0:j1, :],
+                scalar=0.0,
+                in1=acc[:, : (j1 - j0) * P].rearrange("p (j i) -> p j i", i=P),
+                op0=ALU.is_gt,
+                op1=ALU.mult,
+            )
+
+        def project(j0, j1):
+            width = (j1 - j0) * P
+            cols = slice(j0 * P, j1 * P)
+            turned = work.tile([P, 4 * C], F32, name="bank")
+            for j in range(j0, j1):
+                pairs = da_t[:, j, :].bitcast(F32)
+                for u in range(2):
+                    first = u * width + (j - j0) * P
+                    nc.tensor.transpose(turned[:, first : first + P], pairs[:, u : H // 2 : 2], ident[:])
+            nc.scalar.copy(
+                da_bf[:, cols, :].bitcast(F32),
+                turned[:, : 2 * width].rearrange("p (u t) -> p t u", u=2),
+            )
+            nc.vector.quantize_mx(
+                out=da_w[:, cols].bitcast(FP8X4),
+                scales=da_s[:, cols],
+                in_=da_bf[:, cols, :].rearrange("p t d -> p (t d)"),
+            )
+            result = work.tile([P, 4 * C], F32, name="bank")
+            for m in range(K // P):
+                nc.tensor.matmul_mx(
+                    out=result[:, m * width : (m + 1) * width],
+                    lhsT=w1_w[:, m * P : (m + 1) * P].bitcast(FP8X4),
+                    lhsT_scale=w1_s[:, m * P : (m + 1) * P],
+                    rhs=da_w[:, cols].bitcast(FP8X4),
+                    rhs_scale=da_s[:, cols],
+                    start=True,
+                    stop=True,
+                )
+            nc.scalar.copy(res[:, :, cols], result[:, : 2 * width].rearrange("p (m t) -> p m t", m=2))
+            nc.sync.dma_start(out.rearrange("(m p) t -> p m t", p=P)[:, :, cols], res[:, :, cols])
+
+        expert_products(0, FIRST_GROUPS)
+        expert_products(1, GROUPS)
+        expert_products(2, GROUPS)
+        for c in range(HT):
+            turn_a(c)
+        expert_products(3, GROUPS)
+        nc.scalar.copy(w1_bf[:], w1_raw[:].rearrange("p d k -> p k d"))
+
+        for c in range(HT - 1):
+            mask(c, 0, TT, combine(c, 0, TT))
+        nc.vector.quantize_mx(
+            out=w1_w[:].bitcast(FP8X4), scales=w1_s[:], in_=w1_bf[:].rearrange("p k d -> p (k d)")
+        )
+        for j0, j1 in LAST_SPANS:
+            mask(HT - 1, j0, j1, combine(HT - 1, j0, j1))
+        for j0, j1 in OUT_SPANS:
+            project(j0, j1)

@@ -15,6 +15,7 @@ U8 = mybir.dt.uint8
 FP8X4 = mybir.dt.float8_e4m3fn_x4
 FP4X4 = mybir.dt.float4_e2m1fn_x4
 ALU = mybir.AluOpType
+ACT = mybir.ActivationFunctionType
 
 P = 128
 S = E * C
@@ -25,7 +26,6 @@ WORD_PIECES = ((0, 6), (6, 12), (12, 16))
 BYTE_PIECES = ((0, 6), (6, 12), (12, 15), (15, 16))
 FIRST_GROUPS = ((0, 4), (4, 8), (8, 12), (12, 15), (15, 16))
 GROUPS = ((0, 4), (4, 8), (8, 12), (12, 16))
-LAST_SPANS = ((0, 3), (3, 4))
 OUT_SPANS = ((0, 2), (2, 3), (3, 4))
 
 
@@ -42,28 +42,25 @@ def tile_moe_sub_relu_kernel(
         offs_sb = keep.tile([P, S // 16], U16, name="offs_sb")
         pos_sb = [keep.tile([P, T // 16], U16, name=f"pos_sb{r}") for r in range(TOP)]
         dy_w = keep.tile([P, WINDOW], I32, name="dy_w", align_bytes=64)
-        dy_s = keep.tile([P, WINDOW], U8, name="dy_s", align_bytes=64)
+        dy_s = keep.tile([P, WINDOW], U8, name="dy_s", tag="reused", align_bytes=64)
         slot_w = keep.tile([P, S], U32, name="slot_w", align_bytes=64)
         slot_s = keep.tile([P, S], U8, name="slot_s", align_bytes=64)
         w2_w = keep.tile([P, E, 2 * H], U8, name="w2_w", align_bytes=64)
         w2_s = keep.tile([P, E, H], U8, name="w2_s", align_bytes=64)
         gate_sb = keep.tile([P, TOP, T], F32, name="gate_sb")
-        a_sb = keep.tile([P, HT, T], F32, name="a_sb")
-        a_t = keep.tile([P, HT, TT, P], F32, name="a_t")
-        w1_raw = keep.tile([P, 4, K], F32, name="w1_raw")
+        sign = keep.tile([P, T, 4], BF16, name="sign")
+        mask = keep.tile([P, T, 4], BF16, name="mask")
         w1_bf = keep.tile([P, K, 4], BF16, name="w1_bf", align_bytes=64)
         w1_w = keep.tile([P, K], U32, name="w1_w", align_bytes=64)
         w1_s = keep.tile([P, K], U8, name="w1_s", align_bytes=64)
         y = [keep.tile([P, S], F32, name=f"y{c}") for c in range(HT)]
-        da_t = keep.tile([P, TT, H], BF16, name="da_t", align_bytes=64)
+        da_t = keep.tile([P, 2, TT, H // 2], BF16, name="da_t", align_bytes=64)
         da_bf = keep.tile([P, T, 4], BF16, name="da_bf", align_bytes=64)
         da_w = keep.tile([P, T], U32, name="da_w", align_bytes=64)
         da_s = keep.tile([P, T], U8, name="da_s", align_bytes=64)
-        res = keep.tile([P, K // P, T], F32, name="res")
         ident = keep.tile([P, P], F32, name="ident")
 
         nc.vector.memset(dy_s[:].bitcast(I32), 0)
-        nc.vector.memset(w2_s[:].rearrange("p e i -> p (e i)").bitcast(I32), 0)
         nc.vector.memset(dy_w[:, T:], 0)
         make_identity(nc, ident[:])
 
@@ -84,8 +81,6 @@ def tile_moe_sub_relu_kernel(
         for r, pos in enumerate((pos1, pos2, pos3, pos4)):
             nc.sync.dma_start(pos_sb[r][:], pos)
             nc.sync.dma_start(gate_sb[:, r, :], gate[r])
-        nc.sync.dma_start(a_sb[:], a.rearrange("(c p) t -> p c t", p=P))
-        nc.sync.dma_start(w1_raw[:], w1t.rearrange("(p d) k -> p d k", d=4))
 
         for e0, e1 in WORD_PIECES:
             nc.vector.tensor_copy(
@@ -97,6 +92,12 @@ def tile_moe_sub_relu_kernel(
                 slot_s[:, e0 * C : e1 * C],
                 dy_s[:].indirect(offs_sb[:, e0 * C // 16 : e1 * C // 16]),
             )
+
+        late = keep.tile([P, 4 * (T + K)], F32, name="late", tag="reused", align_bytes=64)
+        a_sb = late[:, : 4 * T].rearrange("p (d t) -> p d t", d=4)
+        w1_raw = late[:, 4 * T :].rearrange("p (d k) -> p d k", d=4)
+        nc.sync.dma_start(w1_raw, w1t.rearrange("(p d) k -> p d k", d=4))
+        nc.sync.dma_start(a_sb, a.rearrange("(p d) t -> p d t", d=4))
 
         def expert_products(c, groups):
             for e0, e1 in groups:
@@ -116,61 +117,66 @@ def tile_moe_sub_relu_kernel(
                 else:
                     nc.scalar.copy(y[c][:, e0 * C : e1 * C], bank[:, : (e1 - e0) * C])
 
-        def turn_a(c):
-            bank = work.tile([P, 4 * C], F32, name="bank")
-            for j in range(TT):
-                nc.tensor.transpose(bank[:, j * P : (j + 1) * P], a_sb[:, c, j * P : (j + 1) * P], ident[:])
-            nc.scalar.copy(a_t[:, c].rearrange("p j i -> p (j i)"), bank[:])
-
-        def combine(c, j0, j1):
-            acc = sums.tile([P, T], F32, name="acc")
-            for r in range(TOP):
-                prod = ring.tile([P, T], F32, name="prod")
-                nc.vector.tensor_tensor(
-                    prod[:, : (j1 - j0) * P],
-                    y[c][:].indirect(pos_sb[r][:, j0 * P // 16 : j1 * P // 16]),
-                    gate_sb[:, r, j0 * P : j1 * P],
-                    ALU.mult,
+        def add_choice(acc, c, r, j0, j1):
+            prod = ring.tile([P, T], F32, name="prod")
+            nc.vector.tensor_tensor(
+                prod[:, : (j1 - j0) * P],
+                y[c][:].indirect(pos_sb[r][:, j0 * P // 16 : j1 * P // 16]),
+                gate_sb[:, r, j0 * P : j1 * P],
+                ALU.mult,
+            )
+            for j in range(j1 - j0):
+                nc.tensor.matmul(
+                    acc[:, j * P : (j + 1) * P],
+                    prod[:, j * P : (j + 1) * P],
+                    ident[:],
+                    start=(r == 0 and j == 0),
+                    stop=(r == TOP - 1 and j == j1 - j0 - 1),
+                    is_transpose=True,
                 )
-                for j in range(j1 - j0):
-                    nc.tensor.matmul(
-                        acc[:, j * P : (j + 1) * P],
-                        prod[:, j * P : (j + 1) * P],
-                        ident[:],
-                        start=(r == 0 and j == 0),
-                        stop=(r == TOP - 1 and j == j1 - j0 - 1),
-                        is_transpose=True,
-                    )
-            return acc
 
-        def mask(c, j0, j1, acc):
-            nc.vector.scalar_tensor_tensor(
-                out=da_t[:, j0:j1, c * P : (c + 1) * P],
-                in0=a_t[:, c, j0:j1, :],
-                scalar=0.0,
-                in1=acc[:, : (j1 - j0) * P].rearrange("p (j i) -> p j i", i=P),
-                op0=ALU.is_gt,
-                op1=ALU.mult,
+        def round_sum(acc, first, c, j0, j1):
+            nc.scalar.copy(
+                da_t[:, :, j0:j1, c * P // 2 : (c + 1) * P // 2].rearrange("p u j (q e) -> p u j q e", e=2),
+                acc[:, (j0 - first) * P : (j1 - first) * P].rearrange(
+                    "p (j q u e) -> p u j q e", q=32, u=2, e=2
+                ),
             )
 
-        def project(j0, j1):
-            width = (j1 - j0) * P
-            cols = slice(j0 * P, j1 * P)
+        def make_mask(j):
+            cols = slice(j * P, (j + 1) * P)
+            nc.scalar.activation(sign[:, cols, :], a_sb[:, :, cols].rearrange("p d t -> p t d"), ACT.Sign)
+            nc.scalar.activation(mask[:, cols, :], sign[:, cols, :], ACT.Relu)
+
+        def turn_back(j0, j1):
             turned = work.tile([P, 4 * C], F32, name="bank")
             for j in range(j0, j1):
-                pairs = da_t[:, j, :].bitcast(F32)
+                first = 2 * (j - j0) * P
                 for u in range(2):
-                    first = u * width + (j - j0) * P
-                    nc.tensor.transpose(turned[:, first : first + P], pairs[:, u : H // 2 : 2], ident[:])
-            nc.scalar.copy(
-                da_bf[:, cols, :].bitcast(F32),
-                turned[:, : 2 * width].rearrange("p (u t) -> p t u", u=2),
+                    nc.tensor.transpose(
+                        turned[:, first + u : first + 2 * P : 2], da_t[:, u, j, :].bitcast(F32), ident[:]
+                    )
+            return turned
+
+        def apply_mask(turned, j0, j1):
+            nc.vector.tensor_tensor(
+                da_bf[:, j0 * P : j1 * P, :].rearrange("p t d -> p (t d)"),
+                turned[:, : 2 * (j1 - j0) * P].bitcast(BF16),
+                mask[:, j0 * P : j1 * P, :].rearrange("p t d -> p (t d)"),
+                ALU.mult,
             )
+
+        def quantise_da(j0, j1):
+            cols = slice(j0 * P, j1 * P)
             nc.vector.quantize_mx(
                 out=da_w[:, cols].bitcast(FP8X4),
                 scales=da_s[:, cols],
                 in_=da_bf[:, cols, :].rearrange("p t d -> p (t d)"),
             )
+
+        def project(j0, j1):
+            width = (j1 - j0) * P
+            cols = slice(j0 * P, j1 * P)
             result = work.tile([P, 4 * C], F32, name="bank")
             for m in range(K // P):
                 nc.tensor.matmul_mx(
@@ -182,23 +188,53 @@ def tile_moe_sub_relu_kernel(
                     start=True,
                     stop=True,
                 )
-            nc.scalar.copy(res[:, :, cols], result[:, : 2 * width].rearrange("p (m t) -> p m t", m=2))
-            nc.sync.dma_start(out.rearrange("(m p) t -> p m t", p=P)[:, :, cols], res[:, :, cols])
+            res = keep.tile([P, 2 * width], F32, name=f"res{j0}")
+            if j1 == TT:
+                nc.vector.tensor_copy(res[:], result[:, : 2 * width])
+            else:
+                nc.scalar.copy(res[:], result[:, : 2 * width])
+            nc.sync.dma_start(
+                out.rearrange("(m p) t -> p m t", p=P)[:, :, cols], res[:].rearrange("p (m t) -> p m t", m=2)
+            )
 
         expert_products(0, FIRST_GROUPS)
-        expert_products(1, GROUPS)
-        expert_products(2, GROUPS)
-        for c in range(HT):
-            turn_a(c)
-        expert_products(3, GROUPS)
-        nc.scalar.copy(w1_bf[:], w1_raw[:].rearrange("p d k -> p k d"))
-
+        for c in range(1, HT):
+            expert_products(c, GROUPS)
         for c in range(HT - 1):
-            mask(c, 0, TT, combine(c, 0, TT))
-        nc.vector.quantize_mx(
-            out=w1_w[:].bitcast(FP8X4), scales=w1_s[:], in_=w1_bf[:].rearrange("p k d -> p (k d)")
-        )
-        for j0, j1 in LAST_SPANS:
-            mask(HT - 1, j0, j1, combine(HT - 1, j0, j1))
+            acc = sums.tile([P, T], F32, name="acc")
+            for r in range(TOP):
+                add_choice(acc, c, r, 0, TT)
+            round_sum(acc, 0, c, 0, TT)
+            if c == 0:
+                nc.scalar.copy(w1_bf[:], w1_raw.rearrange("p d k -> p k d"))
+            if c == 1:
+                nc.vector.quantize_mx(
+                    out=w1_w[:].bitcast(FP8X4), scales=w1_s[:], in_=w1_bf[:].rearrange("p k d -> p (k d)")
+                )
+            if c < 2:
+                make_mask(2 * c)
+                make_mask(2 * c + 1)
+
+        c = HT - 1
+        acc = sums.tile([P, T], F32, name="acc")
+        for r in range(TOP):
+            add_choice(acc, c, r, 0, 3)
+        round_sum(acc, 0, c, 0, 2)
+        round_sum(acc, 0, c, 2, 3)
+        acc = sums.tile([P, T], F32, name="acc")
+        add_choice(acc, c, 0, 3, 4)
+        add_choice(acc, c, 1, 3, 4)
+        turned_a = turn_back(0, 2)
+        add_choice(acc, c, 2, 3, 4)
+        turned_b = turn_back(2, 3)
+        add_choice(acc, c, 3, 3, 4)
+        round_sum(acc, 3, c, 3, 4)
+        turned_c = turn_back(3, 4)
+        apply_mask(turned_a, 0, 2)
+        apply_mask(turned_b, 2, 3)
+        quantise_da(0, 2)
+        quantise_da(2, 3)
+        apply_mask(turned_c, 3, 4)
+        quantise_da(3, 4)
         for j0, j1 in OUT_SPANS:
             project(j0, j1)

@@ -26,7 +26,7 @@ WORD_PIECES = ((0, 6), (6, 12), (12, 16))
 BYTE_PIECES = ((0, 6), (6, 12), (12, 15), (15, 16))
 FIRST_GROUPS = ((0, 4), (4, 8), (8, 12), (12, 15), (15, 16))
 GROUPS = ((0, 4), (4, 8), (8, 12), (12, 16))
-OUT_SPANS = ((0, 2), (2, 3), (3, 4))
+LAST_SPANS = ((0, 2), (2, 3), (3, 4))
 
 
 def tile_moe_sub_relu_kernel(
@@ -35,7 +35,7 @@ def tile_moe_sub_relu_kernel(
     nc = tc.nc
     with ExitStack() as ctx:
         keep = ctx.enter_context(tc.tile_pool(name="keep", bufs=1))
-        ring = ctx.enter_context(tc.tile_pool(name="ring", bufs=6))
+        ring = ctx.enter_context(tc.tile_pool(name="ring", bufs=8))
         work = ctx.enter_context(tc.psum_pool(name="work", bufs=6))
         sums = ctx.enter_context(tc.psum_pool(name="sums", bufs=2))
 
@@ -148,39 +148,34 @@ def tile_moe_sub_relu_kernel(
             nc.scalar.activation(sign[:, cols, :], a_sb[:, :, cols].rearrange("p d t -> p t d"), ACT.Sign)
             nc.scalar.activation(mask[:, cols, :], sign[:, cols, :], ACT.Relu)
 
-        def turn_back(j0, j1):
+        def turn_back(j):
             turned = work.tile([P, 4 * C], F32, name="bank")
-            for j in range(j0, j1):
-                first = 2 * (j - j0) * P
-                for u in range(2):
-                    nc.tensor.transpose(
-                        turned[:, first + u : first + 2 * P : 2], da_t[:, u, j, :].bitcast(F32), ident[:]
-                    )
+            for u in range(2):
+                nc.tensor.transpose(turned[:, u * P : (u + 1) * P], da_t[:, u, j, :].bitcast(F32), ident[:])
             return turned
 
-        def apply_mask(turned, j0, j1):
+        def apply_mask(turned, j):
             nc.vector.tensor_tensor(
-                da_bf[:, j0 * P : j1 * P, :].rearrange("p t d -> p (t d)"),
-                turned[:, : 2 * (j1 - j0) * P].bitcast(BF16),
-                mask[:, j0 * P : j1 * P, :].rearrange("p t d -> p (t d)"),
+                da_bf[:, j * P : (j + 1) * P, :].rearrange("p t (u e) -> p t u e", u=2),
+                turned[:, : 2 * P].bitcast(BF16).rearrange("p (u t e) -> p t u e", u=2, e=2),
+                mask[:, j * P : (j + 1) * P, :].rearrange("p t (u e) -> p t u e", u=2),
                 ALU.mult,
             )
 
-        def quantise_da(j0, j1):
-            cols = slice(j0 * P, j1 * P)
+        def quantise_da(j):
+            cols = slice(j * P, (j + 1) * P)
             nc.vector.quantize_mx(
                 out=da_w[:, cols].bitcast(FP8X4),
                 scales=da_s[:, cols],
                 in_=da_bf[:, cols, :].rearrange("p t d -> p (t d)"),
             )
 
-        def project(j0, j1):
-            width = (j1 - j0) * P
-            cols = slice(j0 * P, j1 * P)
+        def project(j):
+            cols = slice(j * P, (j + 1) * P)
             result = work.tile([P, 4 * C], F32, name="bank")
             for m in range(K // P):
                 nc.tensor.matmul_mx(
-                    out=result[:, m * width : (m + 1) * width],
+                    out=result[:, m * P : (m + 1) * P],
                     lhsT=w1_w[:, m * P : (m + 1) * P].bitcast(FP8X4),
                     lhsT_scale=w1_s[:, m * P : (m + 1) * P],
                     rhs=da_w[:, cols].bitcast(FP8X4),
@@ -188,11 +183,11 @@ def tile_moe_sub_relu_kernel(
                     start=True,
                     stop=True,
                 )
-            res = keep.tile([P, 2 * width], F32, name=f"res{j0}")
-            if j1 == TT:
-                nc.vector.tensor_copy(res[:], result[:, : 2 * width])
+            res = keep.tile([P, 2 * P], F32, name=f"res{j}")
+            if j == TT - 1:
+                nc.vector.tensor_copy(res[:], result[:, : 2 * P])
             else:
-                nc.scalar.copy(res[:], result[:, : 2 * width])
+                nc.scalar.copy(res[:], result[:, : 2 * P])
             nc.sync.dma_start(
                 out.rearrange("(m p) t -> p m t", p=P)[:, :, cols], res[:].rearrange("p (m t) -> p m t", m=2)
             )
@@ -216,25 +211,17 @@ def tile_moe_sub_relu_kernel(
                 make_mask(2 * c + 1)
 
         c = HT - 1
-        acc = sums.tile([P, T], F32, name="acc")
-        for r in range(TOP):
-            add_choice(acc, c, r, 0, 3)
-        round_sum(acc, 0, c, 0, 2)
-        round_sum(acc, 0, c, 2, 3)
-        acc = sums.tile([P, T], F32, name="acc")
-        add_choice(acc, c, 0, 3, 4)
-        add_choice(acc, c, 1, 3, 4)
-        turned_a = turn_back(0, 2)
-        add_choice(acc, c, 2, 3, 4)
-        turned_b = turn_back(2, 3)
-        add_choice(acc, c, 3, 3, 4)
-        round_sum(acc, 3, c, 3, 4)
-        turned_c = turn_back(3, 4)
-        apply_mask(turned_a, 0, 2)
-        apply_mask(turned_b, 2, 3)
-        quantise_da(0, 2)
-        quantise_da(2, 3)
-        apply_mask(turned_c, 3, 4)
-        quantise_da(3, 4)
-        for j0, j1 in OUT_SPANS:
-            project(j0, j1)
+        turned = []
+        for j0, j1 in LAST_SPANS:
+            acc = sums.tile([P, T], F32, name="acc")
+            for r in range(TOP):
+                add_choice(acc, c, r, j0, j1)
+            round_sum(acc, j0, c, j0, j1)
+            turned.extend(turn_back(j) for j in range(j0, j1))
+        apply_mask(turned[0], 0)
+        for j in range(1, TT):
+            apply_mask(turned[j], j)
+            quantise_da(j - 1)
+        quantise_da(TT - 1)
+        for j in range(TT):
+            project(j)

@@ -23,8 +23,8 @@ HT = H // P
 TT = T // P
 WINDOW = 2 * T
 WORD_PIECES = ((0, 6), (6, 12), (12, 16))
-BYTE_PIECES = ((0, 6), (6, 12), (12, 15), (15, 16))
-FIRST_GROUPS = ((0, 4), (4, 8), (8, 12), (12, 15), (15, 16))
+FIRST_GROUPS = ((0, 4), (4, 8), (8, 12), (12, 14), (14, 15), (15, 16))
+BANKS = len(FIRST_GROUPS)
 GROUPS = ((0, 4), (4, 8), (8, 12), (12, 16))
 LAST_SPANS = ((0, 2), (2, 3), (3, 4))
 
@@ -36,7 +36,7 @@ def tile_moe_sub_relu_kernel(
     with ExitStack() as ctx:
         keep = ctx.enter_context(tc.tile_pool(name="keep", bufs=1))
         ring = ctx.enter_context(tc.tile_pool(name="ring", bufs=8))
-        work = ctx.enter_context(tc.psum_pool(name="work", bufs=6))
+        work = ctx.enter_context(tc.psum_pool(name="work", bufs=1))
         sums = ctx.enter_context(tc.psum_pool(name="sums", bufs=2))
 
         offs_sb = keep.tile([P, S // 16], U16, name="offs_sb")
@@ -50,6 +50,7 @@ def tile_moe_sub_relu_kernel(
         gate_sb = keep.tile([P, TOP, T], F32, name="gate_sb")
         sign = keep.tile([P, T, 4], BF16, name="sign")
         mask = keep.tile([P, T, 4], BF16, name="mask")
+        w1_raw = keep.tile([P, 4, K], F32, name="w1_raw")
         w1_bf = keep.tile([P, K, 4], BF16, name="w1_bf", align_bytes=64)
         w1_w = keep.tile([P, K], U32, name="w1_w", align_bytes=64)
         w1_s = keep.tile([P, K], U8, name="w1_s", align_bytes=64)
@@ -74,6 +75,8 @@ def tile_moe_sub_relu_kernel(
                 w2t_scales[:, 0, r:16:4, :].rearrange("e q i -> q e i").bitcast(I32),
             )
         for e0, e1 in GROUPS:
+            if e0 == E // 2:
+                nc.sync.dma_start(w1_raw[:], w1t.rearrange("(p d) k -> p d k", d=4))
             nc.sync.dma_start(
                 w2_w[:, e0:e1, :].bitcast(I32),
                 w2t_words[e0:e1, 0].rearrange("e p b -> p e b").bitcast(I32),
@@ -87,21 +90,26 @@ def tile_moe_sub_relu_kernel(
                 slot_w[:, e0 * C : e1 * C],
                 dy_w[:].bitcast(U32).indirect(offs_sb[:, e0 * C // 16 : e1 * C // 16]),
             )
-        for e0, e1 in BYTE_PIECES:
+        for e0, e1 in FIRST_GROUPS:
             nc.vector.tensor_copy(
                 slot_s[:, e0 * C : e1 * C],
                 dy_s[:].indirect(offs_sb[:, e0 * C // 16 : e1 * C // 16]),
             )
 
-        late = keep.tile([P, 4 * (T + K)], F32, name="late", tag="reused", align_bytes=64)
-        a_sb = late[:, : 4 * T].rearrange("p (d t) -> p d t", d=4)
-        w1_raw = late[:, 4 * T :].rearrange("p (d k) -> p d k", d=4)
-        nc.sync.dma_start(w1_raw, w1t.rearrange("(p d) k -> p d k", d=4))
-        nc.sync.dma_start(a_sb, a.rearrange("(p d) t -> p d t", d=4))
+        nc.scalar.copy(w1_bf[:], w1_raw[:].rearrange("p d k -> p k d"))
+        nc.vector.quantize_mx(
+            out=w1_w[:].bitcast(FP8X4), scales=w1_s[:], in_=w1_bf[:].rearrange("p k d -> p (k d)")
+        )
 
-        def expert_products(c, groups):
-            for e0, e1 in groups:
-                bank = work.tile([P, 4 * C], F32, name="bank")
+        a_sb = keep.tile([P, 4, T], F32, name="a_sb", tag="reused", align_bytes=64)
+        nc.sync.dma_start(a_sb[:], a.rearrange("(p d) t -> p d t", d=4))
+
+        def take_bank(b):
+            return work.tile([P, 4 * C], F32, name=f"bank{b}")
+
+        def expert_products(c, groups, banks):
+            for (e0, e1), b in zip(groups, banks):
+                bank = take_bank(b)
                 for e in range(e0, e1):
                     nc.tensor.matmul_mx(
                         out=bank[:, (e - e0) * C : (e - e0 + 1) * C],
@@ -149,7 +157,7 @@ def tile_moe_sub_relu_kernel(
             nc.scalar.activation(mask[:, cols, :], sign[:, cols, :], ACT.Relu)
 
         def turn_back(j):
-            turned = work.tile([P, 4 * C], F32, name="bank")
+            turned = take_bank(j)
             for u in range(2):
                 nc.tensor.transpose(turned[:, u * P : (u + 1) * P], da_t[:, u, j, :].bitcast(F32), ident[:])
             return turned
@@ -172,7 +180,7 @@ def tile_moe_sub_relu_kernel(
 
         def project(j):
             cols = slice(j * P, (j + 1) * P)
-            result = work.tile([P, 4 * C], F32, name="bank")
+            result = take_bank((TT + j) % BANKS)
             for m in range(K // P):
                 nc.tensor.matmul_mx(
                     out=result[:, m * P : (m + 1) * P],
@@ -192,20 +200,14 @@ def tile_moe_sub_relu_kernel(
                 out.rearrange("(m p) t -> p m t", p=P)[:, :, cols], res[:].rearrange("p (m t) -> p m t", m=2)
             )
 
-        expert_products(0, FIRST_GROUPS)
+        expert_products(0, FIRST_GROUPS, range(BANKS))
         for c in range(1, HT):
-            expert_products(c, GROUPS)
+            expert_products(c, GROUPS, (3, 4, 5, c - 1))
         for c in range(HT - 1):
             acc = sums.tile([P, T], F32, name="acc")
             for r in range(TOP):
                 add_choice(acc, c, r, 0, TT)
             round_sum(acc, 0, c, 0, TT)
-            if c == 0:
-                nc.scalar.copy(w1_bf[:], w1_raw.rearrange("p d k -> p k d"))
-            if c == 1:
-                nc.vector.quantize_mx(
-                    out=w1_w[:].bitcast(FP8X4), scales=w1_s[:], in_=w1_bf[:].rearrange("p k d -> p (k d)")
-                )
             if c < 2:
                 make_mask(2 * c)
                 make_mask(2 * c + 1)

@@ -21,8 +21,8 @@ P = 128
 S = E * C
 HT = H // P
 TT = T // P
-WINDOW = 2 * T
-WORD_PIECES = ((0, 6), (6, 12), (12, 16))
+WINDOW = 1408
+WORD_PIECES = ((0, 8), (8, 16))
 FIRST_GROUPS = ((0, 4), (4, 8), (8, 12), (12, 14), (14, 15), (15, 16))
 BANKS = len(FIRST_GROUPS)
 GROUPS = ((0, 4), (4, 8), (8, 12), (12, 16))
@@ -42,7 +42,7 @@ def tile_moe_sub_relu_kernel(
         offs_sb = keep.tile([P, S // 16], U16, name="offs_sb")
         pos_sb = [keep.tile([P, T // 16], U16, name=f"pos_sb{r}") for r in range(TOP)]
         dy_w = keep.tile([P, WINDOW], I32, name="dy_w", align_bytes=64)
-        dy_s = keep.tile([P, WINDOW], U8, name="dy_s", tag="reused", align_bytes=64)
+        dy_s = keep.tile([P, 2 * T], U8, name="dy_s", tag="reused", align_bytes=64)
         slot_w = keep.tile([P, S], U32, name="slot_w", align_bytes=64)
         slot_s = keep.tile([P, S], U8, name="slot_s", align_bytes=64)
         w2_w = keep.tile([P, E, 2 * H], U8, name="w2_w", align_bytes=64)
@@ -65,8 +65,8 @@ def tile_moe_sub_relu_kernel(
         nc.vector.memset(dy_w[:, T:], 0)
         make_identity(nc, ident[:])
 
-        nc.sync.dma_start(offs_sb[:], offs)
         nc.sync.dma_start(dy_w[:, :T], dy_words[0].rearrange("p t d -> p (t d)").bitcast(I32))
+        nc.sync.dma_start(offs_sb[:], offs)
         for r in range(4):
             nc.sync.dma_start(dy_s[r:P:32, :T].bitcast(I32), dy_scales[0, r:16:4, :].bitcast(I32))
         for r in range(4):
@@ -180,10 +180,12 @@ def tile_moe_sub_relu_kernel(
 
         def project(j):
             cols = slice(j * P, (j + 1) * P)
+            last = j == TT - 1
             result = take_bank((TT + j) % BANKS)
+            halves = [result[:, :P], take_bank((TT + j + 1) % BANKS)[:, :P] if last else result[:, P : 2 * P]]
             for m in range(K // P):
                 nc.tensor.matmul_mx(
-                    out=result[:, m * P : (m + 1) * P],
+                    out=halves[m],
                     lhsT=w1_w[:, m * P : (m + 1) * P].bitcast(FP8X4),
                     lhsT_scale=w1_s[:, m * P : (m + 1) * P],
                     rhs=da_w[:, cols].bitcast(FP8X4),
@@ -192,8 +194,9 @@ def tile_moe_sub_relu_kernel(
                     stop=True,
                 )
             res = keep.tile([P, 2 * P], F32, name=f"res{j}")
-            if j == TT - 1:
-                nc.vector.tensor_copy(res[:], result[:, : 2 * P])
+            if last:
+                for m in range(K // P):
+                    nc.vector.tensor_copy(res[:, m * P : (m + 1) * P], halves[m])
             else:
                 nc.scalar.copy(res[:], result[:, : 2 * P])
             nc.sync.dma_start(

@@ -68,7 +68,7 @@ def tile_moe_sub_relu_kernel(
         nc.sync.dma_start(dy_w[:, :T], dy_words[0].rearrange("p t d -> p (t d)").bitcast(I32))
         nc.sync.dma_start(offs_sb[:], offs)
         for r in range(4):
-            nc.sync.dma_start(dy_s[r:P:32, :T].bitcast(I32), dy_scales[0, r:16:4, :].bitcast(I32))
+            nc.scalar.dma_start(dy_s[r:P:32, :T].bitcast(I32), dy_scales[0, r:16:4, :].bitcast(I32))
         for r in range(4):
             nc.sync.dma_start(
                 w2_s[r:P:32, :, :].bitcast(I32),

@@ -23,7 +23,7 @@ HT = H // P
 TT = T // P
 WINDOW = 1408
 WORD_PIECES = ((0, 8), (8, 16))
-FIRST_GROUPS = ((0, 4), (4, 8), (8, 12), (12, 14), (14, 15), (15, 16))
+FIRST_GROUPS = ((0, 4), (4, 8), (8, 11), (11, 13), (13, 15), (15, 16))
 BANKS = len(FIRST_GROUPS)
 GROUPS = ((0, 4), (4, 8), (8, 12), (12, 16))
 LAST_SPANS = ((0, 2), (2, 3), (3, 4))
@@ -69,18 +69,18 @@ def tile_moe_sub_relu_kernel(
         nc.sync.dma_start(offs_sb[:], offs)
         for r in range(4):
             nc.scalar.dma_start(dy_s[r:P:32, :T].bitcast(I32), dy_scales[0, r:16:4, :].bitcast(I32))
-        for r in range(4):
-            nc.sync.dma_start(
-                w2_s[r:P:32, :, :].bitcast(I32),
-                w2t_scales[:, 0, r:16:4, :].rearrange("e q i -> q e i").bitcast(I32),
-            )
+        nc.sync.dma_start(w1_raw[:], w1t.rearrange("(p d) k -> p d k", d=4))
         for e0, e1 in GROUPS:
-            if e0 == E // 2:
-                nc.sync.dma_start(w1_raw[:], w1t.rearrange("(p d) k -> p d k", d=4))
             nc.sync.dma_start(
                 w2_w[:, e0:e1, :].bitcast(I32),
                 w2t_words[e0:e1, 0].rearrange("e p b -> p e b").bitcast(I32),
             )
+            if e0 == 0:
+                for r in range(4):
+                    nc.sync.dma_start(
+                        w2_s[r:P:32, :, :].bitcast(I32),
+                        w2t_scales[:, 0, r:16:4, :].rearrange("e q i -> q e i").bitcast(I32),
+                    )
         for r, pos in enumerate((pos1, pos2, pos3, pos4)):
             nc.sync.dma_start(pos_sb[r][:], pos)
             nc.sync.dma_start(gate_sb[:, r, :], gate[r])

@@ -1,7 +1,6 @@
 from contextlib import ExitStack
 
 import concourse.mybir as mybir
-from concourse.masks import make_identity
 
 K, T, E, C, H, N, TOP = 256, 512, 16, 128, 512, 512, 4
 FLOPS = 2 * N * H * E * C + 2 * H * K * T
@@ -23,6 +22,7 @@ HT = H // P
 TT = T // P
 WINDOW = 1408
 WORD_PIECES = ((0, 8), (8, 16))
+BYTE_PIECES = ((0, 6), (6, 11), (11, 13), (13, 15), (15, 16))
 FIRST_GROUPS = ((0, 4), (4, 8), (8, 11), (11, 13), (13, 15), (15, 16))
 BANKS = len(FIRST_GROUPS)
 GROUPS = ((0, 4), (4, 8), (8, 12), (12, 16))
@@ -35,6 +35,7 @@ def tile_moe_sub_relu_kernel(
     nc = tc.nc
     with ExitStack() as ctx:
         keep = ctx.enter_context(tc.tile_pool(name="keep", bufs=1))
+        shared = ctx.enter_context(tc.tile_pool(name="shared", bufs=1))
         ring = ctx.enter_context(tc.tile_pool(name="ring", bufs=8))
         work = ctx.enter_context(tc.psum_pool(name="work", bufs=1))
         sums = ctx.enter_context(tc.psum_pool(name="sums", bufs=2))
@@ -42,7 +43,7 @@ def tile_moe_sub_relu_kernel(
         offs_sb = keep.tile([P, S // 16], U16, name="offs_sb")
         pos_sb = [keep.tile([P, T // 16], U16, name=f"pos_sb{r}") for r in range(TOP)]
         dy_w = keep.tile([P, WINDOW], I32, name="dy_w", align_bytes=64)
-        dy_s = keep.tile([P, 2 * T], U8, name="dy_s", tag="reused", align_bytes=64)
+        dy_s = shared.tile([P, 2 * T], U8, name="dy_s", offset=16 * T - T, align_bytes=64)
         slot_w = keep.tile([P, S], U32, name="slot_w", align_bytes=64)
         slot_s = keep.tile([P, S], U8, name="slot_s", align_bytes=64)
         w2_w = keep.tile([P, E, 2 * H], U8, name="w2_w", align_bytes=64)
@@ -59,11 +60,11 @@ def tile_moe_sub_relu_kernel(
         da_bf = keep.tile([P, T, 4], BF16, name="da_bf", align_bytes=64)
         da_w = keep.tile([P, T], U32, name="da_w", align_bytes=64)
         da_s = keep.tile([P, T], U8, name="da_s", align_bytes=64)
-        ident = keep.tile([P, P], F32, name="ident")
+        zeros = keep.tile([P, P], F32, name="zeros")
 
         nc.vector.memset(dy_s[:].bitcast(I32), 0)
         nc.vector.memset(dy_w[:, T:], 0)
-        make_identity(nc, ident[:])
+        nc.vector.memset(zeros[:], 0.0)
 
         nc.sync.dma_start(dy_w[:, :T], dy_words[0].rearrange("p t d -> p (t d)").bitcast(I32))
         nc.sync.dma_start(offs_sb[:], offs)
@@ -90,18 +91,29 @@ def tile_moe_sub_relu_kernel(
                 slot_w[:, e0 * C : e1 * C],
                 dy_w[:].bitcast(U32).indirect(offs_sb[:, e0 * C // 16 : e1 * C // 16]),
             )
-        for e0, e1 in FIRST_GROUPS:
+        for e0, e1 in BYTE_PIECES:
             nc.vector.tensor_copy(
                 slot_s[:, e0 * C : e1 * C],
                 dy_s[:].indirect(offs_sb[:, e0 * C // 16 : e1 * C // 16]),
             )
+
+        ident = shared.tile([P, P], F32, name="ident", offset=16 * T, align_bytes=64)
+        nc.gpsimd.affine_select(
+            out=ident[:],
+            in_=zeros[:],
+            compare_op=ALU.not_equal,
+            fill=1.0,
+            base=0,
+            pattern=[[-1, P]],
+            channel_multiplier=1,
+        )
 
         nc.scalar.copy(w1_bf[:], w1_raw[:].rearrange("p d k -> p k d"))
         nc.vector.quantize_mx(
             out=w1_w[:].bitcast(FP8X4), scales=w1_s[:], in_=w1_bf[:].rearrange("p k d -> p (k d)")
         )
 
-        a_sb = keep.tile([P, 4, T], F32, name="a_sb", tag="reused", align_bytes=64)
+        a_sb = shared.tile([P, 4, T], F32, name="a_sb", offset=0, align_bytes=64)
         nc.sync.dma_start(a_sb[:], a.rearrange("(p d) t -> p d t", d=4))
 
         def take_bank(b):

@@ -36,7 +36,6 @@ def tile_moe_sub_relu_kernel(
     with ExitStack() as ctx:
         keep = ctx.enter_context(tc.tile_pool(name="keep", bufs=1))
         shared = ctx.enter_context(tc.tile_pool(name="shared", bufs=1))
-        ring = ctx.enter_context(tc.tile_pool(name="ring", bufs=8))
         work = ctx.enter_context(tc.psum_pool(name="work", bufs=1))
         sums = ctx.enter_context(tc.psum_pool(name="sums", bufs=2))
 
@@ -138,7 +137,7 @@ def tile_moe_sub_relu_kernel(
                     nc.scalar.copy(y[c][:, e0 * C : e1 * C], bank[:, : (e1 - e0) * C])
 
         def add_choice(acc, c, r, j0, j1):
-            prod = ring.tile([P, T], F32, name="prod")
+            prod = keep.tile([P, (j1 - j0) * P], F32, name=f"prod{c}_{r}_{j0}")
             nc.vector.tensor_tensor(
                 prod[:, : (j1 - j0) * P],
                 y[c][:].indirect(pos_sb[r][:, j0 * P // 16 : j1 * P // 16]),

@@ -20,12 +20,11 @@ P = 128
 S = E * C
 HT = H // P
 TT = T // P
-WINDOW = 1408
-WORD_PIECES = ((0, 8), (8, 16))
-BYTE_PIECES = ((0, 6), (6, 11), (11, 13), (13, 15), (15, 16))
-FIRST_GROUPS = ((0, 4), (4, 8), (8, 11), (11, 13), (13, 15), (15, 16))
-BANKS = len(FIRST_GROUPS)
-GROUPS = ((0, 4), (4, 8), (8, 12), (12, 16))
+PIECES = ((0, 3), (3, 6), (6, 9), (9, 12), (12, 15), (15, 16))
+FIRST = PIECES[0][1]
+LOADS = ((0, 3), (3, 6), (6, 11), (11, 16))
+SCALE_LOADS = {0: ((0, 3),), 3: ((3, 16),)}
+RING = 6
 LAST_SPANS = ((0, 2), (2, 3), (3, 4))
 
 
@@ -36,22 +35,21 @@ def tile_moe_sub_relu_kernel(
     with ExitStack() as ctx:
         keep = ctx.enter_context(tc.tile_pool(name="keep", bufs=1))
         shared = ctx.enter_context(tc.tile_pool(name="shared", bufs=1))
-        work = ctx.enter_context(tc.psum_pool(name="work", bufs=1))
-        sums = ctx.enter_context(tc.psum_pool(name="sums", bufs=2))
+        held = ctx.enter_context(tc.tile_pool(name="held", bufs=1))
+        psum = ctx.enter_context(tc.psum_pool(name="psum", bufs=1))
 
         offs_sb = keep.tile([P, S // 16], U16, name="offs_sb")
         pos_sb = [keep.tile([P, T // 16], U16, name=f"pos_sb{r}") for r in range(TOP)]
-        dy_w = keep.tile([P, WINDOW], I32, name="dy_w", align_bytes=64)
-        dy_s = shared.tile([P, 2 * T], U8, name="dy_s", offset=16 * T - T, align_bytes=64)
-        slot_w = keep.tile([P, S], U32, name="slot_w", align_bytes=64)
+        dy_w = keep.tile([P, T], I32, name="dy_w", align_bytes=64)
+        dy_s0 = shared.tile([P, T], U8, name="dy_s0", offset=T, align_bytes=64)
+        dy_s = shared.tile([P, T], U8, name="dy_s", offset=0, align_bytes=64)
+        first_w = keep.tile([P, FIRST * C], U32, name="first_w", align_bytes=64)
         slot_s = keep.tile([P, S], U8, name="slot_s", align_bytes=64)
         w2_w = keep.tile([P, E, 2 * H], U8, name="w2_w", align_bytes=64)
         w2_s = keep.tile([P, E, H], U8, name="w2_s", align_bytes=64)
         gate_sb = keep.tile([P, TOP, T], F32, name="gate_sb")
-        sign = keep.tile([P, T, 4], BF16, name="sign")
-        mask = keep.tile([P, T, 4], BF16, name="mask")
+        a_sb = keep.tile([P, 4, T], F32, name="a_sb")
         w1_raw = keep.tile([P, 4, K], F32, name="w1_raw")
-        w1_bf = keep.tile([P, K, 4], BF16, name="w1_bf", align_bytes=64)
         w1_w = keep.tile([P, K], U32, name="w1_w", align_bytes=64)
         w1_s = keep.tile([P, K], U8, name="w1_s", align_bytes=64)
         y = [keep.tile([P, S], F32, name=f"y{c}") for c in range(HT)]
@@ -61,42 +59,55 @@ def tile_moe_sub_relu_kernel(
         da_s = keep.tile([P, T], U8, name="da_s", align_bytes=64)
         zeros = keep.tile([P, P], F32, name="zeros")
 
-        nc.vector.memset(dy_s[:].bitcast(I32), 0)
-        nc.vector.memset(dy_w[:, T:], 0)
+        nc.vector.memset(dy_s0[:].bitcast(I32), 0)
         nc.vector.memset(zeros[:], 0.0)
 
-        nc.sync.dma_start(dy_w[:, :T], dy_words[0].rearrange("p t d -> p (t d)").bitcast(I32))
+        nc.sync.dma_start(dy_w[:], dy_words[0].rearrange("p t d -> p (t d)").bitcast(I32))
         nc.sync.dma_start(offs_sb[:], offs)
         for r in range(4):
-            nc.scalar.dma_start(dy_s[r:P:32, :T].bitcast(I32), dy_scales[0, r:16:4, :].bitcast(I32))
-        nc.sync.dma_start(w1_raw[:], w1t.rearrange("(p d) k -> p d k", d=4))
-        for e0, e1 in GROUPS:
+            nc.scalar.dma_start(dy_s0[r:P:32, :].bitcast(I32), dy_scales[0, r:16:4, :].bitcast(I32))
+        for e0, e1 in LOADS:
+            for s0, s1 in SCALE_LOADS.get(e0, ()):
+                for r in range(4):
+                    nc.sync.dma_start(
+                        w2_s[r:P:32, s0:s1, :].bitcast(I32),
+                        w2t_scales[s0:s1, 0, r:16:4, :].rearrange("e q i -> q e i").bitcast(I32),
+                    )
             nc.sync.dma_start(
                 w2_w[:, e0:e1, :].bitcast(I32),
                 w2t_words[e0:e1, 0].rearrange("e p b -> p e b").bitcast(I32),
             )
-            if e0 == 0:
-                for r in range(4):
-                    nc.sync.dma_start(
-                        w2_s[r:P:32, :, :].bitcast(I32),
-                        w2t_scales[:, 0, r:16:4, :].rearrange("e q i -> q e i").bitcast(I32),
-                    )
         for r, pos in enumerate((pos1, pos2, pos3, pos4)):
             nc.sync.dma_start(pos_sb[r][:], pos)
+        nc.sync.dma_start(w1_raw[:], w1t.rearrange("(p d) k -> p d k", d=4))
+        for r in range(TOP):
             nc.sync.dma_start(gate_sb[:, r, :], gate[r])
+        nc.sync.dma_start(a_sb[:], a.rearrange("(p d) t -> p d t", d=4))
 
-        for e0, e1 in WORD_PIECES:
+        entries = offs_sb[:, : FIRST * C // 16]
+        nc.vector.tensor_copy(first_w[:], dy_w[:].bitcast(U32).indirect(entries))
+        nc.vector.tensor_copy(slot_s[:, : FIRST * C], dy_s0[:].indirect(entries))
+        nc.vector.tensor_copy(dy_s[:].bitcast(I32), dy_s0[:].bitcast(I32))
+        later_w = shared.tile([P, S - FIRST * C], U32, name="later_w", offset=T, align_bytes=64)
+        for e0, e1 in PIECES[1:]:
+            entries = offs_sb[:, e0 * C // 16 : e1 * C // 16]
             nc.vector.tensor_copy(
-                slot_w[:, e0 * C : e1 * C],
-                dy_w[:].bitcast(U32).indirect(offs_sb[:, e0 * C // 16 : e1 * C // 16]),
+                later_w[:, (e0 - FIRST) * C : (e1 - FIRST) * C], dy_w[:].bitcast(U32).indirect(entries)
             )
-        for e0, e1 in BYTE_PIECES:
-            nc.vector.tensor_copy(
-                slot_s[:, e0 * C : e1 * C],
-                dy_s[:].indirect(offs_sb[:, e0 * C // 16 : e1 * C // 16]),
-            )
+            nc.vector.tensor_copy(slot_s[:, e0 * C : e1 * C], dy_s[:].indirect(entries))
 
-        ident = shared.tile([P, P], F32, name="ident", offset=16 * T, align_bytes=64)
+        def slot_words(e):
+            if e < FIRST:
+                return first_w[:, e * C : (e + 1) * C]
+            return later_w[:, (e - FIRST) * C : (e - FIRST + 1) * C]
+
+        w1_bf = keep.tile([P, K, 4], BF16, name="w1_bf", align_bytes=64)
+        nc.vector.tensor_copy(w1_bf[:], w1_raw[:].rearrange("p d k -> p k d"))
+        nc.vector.quantize_mx(
+            out=w1_w[:].bitcast(FP8X4), scales=w1_s[:], in_=w1_bf[:].rearrange("p k d -> p (k d)")
+        )
+
+        ident = shared.tile([P, P], F32, name="ident", offset=0, align_bytes=64)
         nc.gpsimd.affine_select(
             out=ident[:],
             in_=zeros[:],
@@ -107,68 +118,73 @@ def tile_moe_sub_relu_kernel(
             channel_multiplier=1,
         )
 
-        nc.scalar.copy(w1_bf[:], w1_raw[:].rearrange("p d k -> p k d"))
-        nc.vector.quantize_mx(
-            out=w1_w[:].bitcast(FP8X4), scales=w1_s[:], in_=w1_bf[:].rearrange("p k d -> p (k d)")
-        )
-
-        a_sb = shared.tile([P, 4, T], F32, name="a_sb", offset=0, align_bytes=64)
-        nc.sync.dma_start(a_sb[:], a.rearrange("(p d) t -> p d t", d=4))
-
         def take_bank(b):
-            return work.tile([P, 4 * C], F32, name=f"bank{b}")
+            return psum.tile([P, 4 * C], F32, name=f"bank{b}")
 
-        def expert_products(c, groups, banks):
-            for (e0, e1), b in zip(groups, banks):
-                bank = take_bank(b)
-                for e in range(e0, e1):
-                    nc.tensor.matmul_mx(
-                        out=bank[:, (e - e0) * C : (e - e0 + 1) * C],
-                        lhsT=w2_w[:, e, 2 * P * c : 2 * P * (c + 1)].bitcast(FP4X4),
-                        lhsT_scale=w2_s[:, e, P * c : P * (c + 1)],
-                        rhs=slot_w[:, e * C : (e + 1) * C].bitcast(FP8X4),
-                        rhs_scale=slot_s[:, e * C : (e + 1) * C],
-                        start=True,
-                        stop=True,
-                    )
-                if e1 - e0 == 1:
-                    nc.vector.tensor_copy(y[c][:, e0 * C : e1 * C], bank[:, :C])
-                else:
-                    nc.scalar.copy(y[c][:, e0 * C : e1 * C], bank[:, : (e1 - e0) * C])
+        def expert_products(c, e0, e1, b):
+            bank = take_bank(b)
+            for e in range(e0, e1):
+                nc.tensor.matmul_mx(
+                    out=bank[:, (e - e0) * C : (e - e0 + 1) * C],
+                    lhsT=w2_w[:, e, 2 * P * c : 2 * P * (c + 1)].bitcast(FP4X4),
+                    lhsT_scale=w2_s[:, e, P * c : P * (c + 1)],
+                    rhs=slot_words(e).bitcast(FP8X4),
+                    rhs_scale=slot_s[:, e * C : (e + 1) * C],
+                    start=True,
+                    stop=True,
+                )
+            if c == 0 and e1 == E:
+                nc.vector.tensor_copy(y[c][:, e0 * C : e1 * C], bank[:, : (e1 - e0) * C])
+            else:
+                nc.scalar.activation(y[c][:, e0 * C : e1 * C], bank[:, : (e1 - e0) * C], ACT.Copy)
 
-        def add_choice(acc, c, r, j0, j1):
-            prod = keep.tile([P, (j1 - j0) * P], F32, name=f"prod{c}_{r}_{j0}")
+        steps = [(c, piece) for piece in PIECES[:3] for c in range(HT)]
+        steps.extend(((0, (9, 12)), (1, (9, 12)), (0, (12, 15)), (2, (9, 12)), (3, (9, 12)), (0, (15, 16))))
+        steps.extend((c, (12, 16)) for c in range(1, HT))
+        for n, (c, (e0, e1)) in enumerate(steps):
+            expert_products(c, e0, e1, n % RING)
+
+        def place(n, j0, j1, name):
+            return held.tile([P, (j1 - j0) * P], F32, name=name, offset=4 * (n * T + j0 * P))
+
+        def gather_gated(prod, c, r, j0, j1):
             nc.vector.tensor_tensor(
-                prod[:, : (j1 - j0) * P],
+                prod[:],
                 y[c][:].indirect(pos_sb[r][:, j0 * P // 16 : j1 * P // 16]),
                 gate_sb[:, r, j0 * P : j1 * P],
                 ALU.mult,
             )
-            for j in range(j1 - j0):
+            return prod
+
+        def gather_plain(c, r):
+            picked = place(TOP * c + r, 0, TT, f"picked{c}_{r}")
+            nc.scalar.activation(picked[:], y[c][:].indirect(pos_sb[r][:]), ACT.Copy)
+            return picked
+
+        def apply_gate(picked, c, r):
+            prod = keep.tile([P, T], F32, name=f"prod{c}_{r}")
+            nc.vector.tensor_tensor(prod[:], picked[:], gate_sb[:, r, :], ALU.mult)
+            return prod
+
+        def add_up(acc, prod, first, j0, j1, start, stop):
+            for j in range(j0, j1):
                 nc.tensor.matmul(
-                    acc[:, j * P : (j + 1) * P],
-                    prod[:, j * P : (j + 1) * P],
+                    acc[:, (j - j0) * P : (j - j0 + 1) * P],
+                    prod[:, (j - first) * P : (j - first + 1) * P],
                     ident[:],
-                    start=(r == 0 and j == 0),
-                    stop=(r == TOP - 1 and j == j1 - j0 - 1),
+                    start=(start and j == j0),
+                    stop=(stop and j == j1 - 1),
                     is_transpose=True,
                 )
 
-        def round_sum(acc, first, c, j0, j1):
+        def round_sum(acc, c, j0, j1):
             nc.scalar.copy(
                 da_t[:, :, j0:j1, c * P // 2 : (c + 1) * P // 2].rearrange("p u j (q e) -> p u j q e", e=2),
-                acc[:, (j0 - first) * P : (j1 - first) * P].rearrange(
-                    "p (j q u e) -> p u j q e", q=32, u=2, e=2
-                ),
+                acc[:, : (j1 - j0) * P].rearrange("p (j q u e) -> p u j q e", q=32, u=2, e=2),
             )
 
-        def make_mask(j):
-            cols = slice(j * P, (j + 1) * P)
-            nc.scalar.activation(sign[:, cols, :], a_sb[:, :, cols].rearrange("p d t -> p t d"), ACT.Sign)
-            nc.scalar.activation(mask[:, cols, :], sign[:, cols, :], ACT.Relu)
-
         def turn_back(j):
-            turned = take_bank(j)
+            turned = take_bank(TT + j)
             for u in range(2):
                 nc.tensor.transpose(turned[:, u * P : (u + 1) * P], da_t[:, u, j, :].bitcast(F32), ident[:])
             return turned
@@ -177,7 +193,7 @@ def tile_moe_sub_relu_kernel(
             nc.vector.tensor_tensor(
                 da_bf[:, j * P : (j + 1) * P, :].rearrange("p t (u e) -> p t u e", u=2),
                 turned[:, : 2 * P].bitcast(BF16).rearrange("p (u t e) -> p t u e", u=2, e=2),
-                mask[:, j * P : (j + 1) * P, :].rearrange("p t (u e) -> p t u e", u=2),
+                mask[:, :, j * P : (j + 1) * P, :].rearrange("p u t e -> p t u e"),
                 ALU.mult,
             )
 
@@ -192,8 +208,8 @@ def tile_moe_sub_relu_kernel(
         def project(j):
             cols = slice(j * P, (j + 1) * P)
             last = j == TT - 1
-            result = take_bank((TT + j) % BANKS)
-            halves = [result[:, :P], take_bank((TT + j + 1) % BANKS)[:, :P] if last else result[:, P : 2 * P]]
+            result = take_bank(j)
+            halves = [result[:, :P], take_bank(TT)[:, :P] if last else result[:, P : 2 * P]]
             for m in range(K // P):
                 nc.tensor.matmul_mx(
                     out=halves[m],
@@ -214,25 +230,43 @@ def tile_moe_sub_relu_kernel(
                 out.rearrange("(m p) t -> p m t", p=P)[:, :, cols], res[:].rearrange("p (m t) -> p m t", m=2)
             )
 
-        expert_products(0, FIRST_GROUPS, range(BANKS))
-        for c in range(1, HT):
-            expert_products(c, GROUPS, (3, 4, 5, c - 1))
-        for c in range(HT - 1):
-            acc = sums.tile([P, T], F32, name="acc")
-            for r in range(TOP):
-                add_choice(acc, c, r, 0, TT)
-            round_sum(acc, 0, c, 0, TT)
-            if c < 2:
-                make_mask(2 * c)
-                make_mask(2 * c + 1)
+        acc = take_bank(RING)
+        picked = gather_plain(0, TOP - 1)
+        for r in range(TOP - 1):
+            add_up(acc, gather_gated(place(r, 0, TT, f"gated0_{r}"), 0, r, 0, TT), 0, 0, TT, r == 0, False)
+        add_up(acc, apply_gate(picked, 0, TOP - 1), 0, 0, TT, False, True)
+        for c in range(1, HT - 1):
+            picked = [gather_plain(c, r) for r in range(1, TOP)]
+            round_sum(acc, c - 1, 0, TT)
+            acc = take_bank((RING + c) % 8)
+            prod = place(TOP * c - 1, 0, TT, f"gated{c}_0")
+            add_up(acc, gather_gated(prod, c, 0, 0, TT), 0, 0, TT, True, False)
+            if c == 1:
+                mask = keep.tile([P, 2, T, 2], BF16, name="y0")
+                nc.vector.tensor_scalar(
+                    mask[:], a_sb[:].rearrange("p (u e) t -> p u t e", u=2), 0.0, None, ALU.is_gt
+                )
+            for r in range(1, TOP):
+                add_up(acc, apply_gate(picked[r - 1], c, r), 0, 0, TT, False, r == TOP - 1)
 
         c = HT - 1
+        picked = [gather_plain(c, r) for r in range(2)]
+        round_sum(acc, c - 1, 0, TT)
+        accs = [take_bank(1 + n) for n in range(len(LAST_SPANS))]
+        for r in (2, 3):
+            prod = place(TOP * c - 1, 2 * r - 4, 2 * r - 2, f"gated{c}_{r}_0")
+            add_up(accs[0], gather_gated(prod, c, r, 0, 2), 0, 0, 2, r == 2, False)
+        for r in range(2):
+            prod = apply_gate(picked[r], c, r)
+            for n, (acc, (j0, j1)) in enumerate(zip(accs, LAST_SPANS)):
+                add_up(acc, prod, 0, j0, j1, r == 0 and n > 0, r == 1 and n == 0)
         turned = []
-        for j0, j1 in LAST_SPANS:
-            acc = sums.tile([P, T], F32, name="acc")
-            for r in range(TOP):
-                add_choice(acc, c, r, j0, j1)
-            round_sum(acc, j0, c, j0, j1)
+        for n, (acc, (j0, j1)) in enumerate(zip(accs, LAST_SPANS)):
+            for r in (2, 3) if n > 0 else ():
+                k = 2 * (n - 1) + r - 2
+                prod = place(TOP * c + 1, k, k + 1, f"gated{c}_{r}_{j0}")
+                add_up(acc, gather_gated(prod, c, r, j0, j1), j0, j0, j1, False, r == TOP - 1)
+            round_sum(acc, c, j0, j1)
             turned.extend(turn_back(j) for j in range(j0, j1))
         apply_mask(turned[0], 0)
         for j in range(1, TT):

@@ -22,8 +22,6 @@ HT = H // P
 TT = T // P
 PIECES = ((0, 3), (3, 6), (6, 9), (9, 12), (12, 15), (15, 16))
 FIRST = PIECES[0][1]
-LOADS = ((0, 3), (3, 6), (6, 11), (11, 16))
-SCALE_LOADS = {0: ((0, 3),), 3: ((3, 16),)}
 RING = 6
 LAST_SPANS = ((0, 2), (2, 3), (3, 4))
 
@@ -65,21 +63,30 @@ def tile_moe_sub_relu_kernel(
         nc.sync.dma_start(dy_w[:], dy_words[0].rearrange("p t d -> p (t d)").bitcast(I32))
         nc.sync.dma_start(offs_sb[:], offs)
         for r in range(4):
-            nc.scalar.dma_start(dy_s0[r:P:32, :].bitcast(I32), dy_scales[0, r:16:4, :].bitcast(I32))
-        for e0, e1 in LOADS:
-            for s0, s1 in SCALE_LOADS.get(e0, ()):
-                for r in range(4):
-                    nc.sync.dma_start(
-                        w2_s[r:P:32, s0:s1, :].bitcast(I32),
-                        w2t_scales[s0:s1, 0, r:16:4, :].rearrange("e q i -> q e i").bitcast(I32),
-                    )
+            nc.sync.dma_start(dy_s0[r:P:32, :].bitcast(I32), dy_scales[0, r:16:4, :].bitcast(I32))
+
+        def load_words(e0, e1):
             nc.sync.dma_start(
                 w2_w[:, e0:e1, :].bitcast(I32),
                 w2t_words[e0:e1, 0].rearrange("e p b -> p e b").bitcast(I32),
             )
+
+        def load_scales(e0, e1):
+            for r in range(4):
+                nc.sync.dma_start(
+                    w2_s[r:P:32, e0:e1, :].bitcast(I32),
+                    w2t_scales[e0:e1, 0, r:16:4, :].rearrange("e q i -> q e i").bitcast(I32),
+                )
+
+        load_words(0, 3)
+        nc.sync.dma_start(w1_raw[:], w1t.rearrange("(p d) k -> p d k", d=4))
+        load_scales(0, 6)
+        load_words(3, 6)
+        load_scales(6, 16)
+        load_words(6, 11)
+        load_words(11, 16)
         for r, pos in enumerate((pos1, pos2, pos3, pos4)):
             nc.sync.dma_start(pos_sb[r][:], pos)
-        nc.sync.dma_start(w1_raw[:], w1t.rearrange("(p d) k -> p d k", d=4))
         for r in range(TOP):
             nc.sync.dma_start(gate_sb[:, r, :], gate[r])
         nc.sync.dma_start(a_sb[:], a.rearrange("(p d) t -> p d t", d=4))
@@ -102,7 +109,7 @@ def tile_moe_sub_relu_kernel(
             return later_w[:, (e - FIRST) * C : (e - FIRST + 1) * C]
 
         w1_bf = keep.tile([P, K, 4], BF16, name="w1_bf", align_bytes=64)
-        nc.vector.tensor_copy(w1_bf[:], w1_raw[:].rearrange("p d k -> p k d"))
+        nc.scalar.copy(w1_bf[:], w1_raw[:].rearrange("p d k -> p k d"))
         nc.vector.quantize_mx(
             out=w1_w[:].bitcast(FP8X4), scales=w1_s[:], in_=w1_bf[:].rearrange("p k d -> p (k d)")
         )
@@ -133,13 +140,13 @@ def tile_moe_sub_relu_kernel(
                     start=True,
                     stop=True,
                 )
-            if c == 0 and e1 == E:
+            if c == 0 and e0 >= 12:
                 nc.vector.tensor_copy(y[c][:, e0 * C : e1 * C], bank[:, : (e1 - e0) * C])
             else:
                 nc.scalar.activation(y[c][:, e0 * C : e1 * C], bank[:, : (e1 - e0) * C], ACT.Copy)
 
         steps = [(c, piece) for piece in PIECES[:3] for c in range(HT)]
-        steps.extend(((0, (9, 12)), (1, (9, 12)), (0, (12, 15)), (2, (9, 12)), (3, (9, 12)), (0, (15, 16))))
+        steps.extend(((0, (9, 12)), (1, (9, 12)), (2, (9, 12)), (3, (9, 12)), (0, (12, 15)), (0, (15, 16))))
         steps.extend((c, (12, 16)) for c in range(1, HT))
         for n, (c, (e0, e1)) in enumerate(steps):
             expert_products(c, e0, e1, n % RING)

@@ -47,7 +47,7 @@ def tile_moe_sub_relu_kernel(
         w2_s = keep.tile([P, E, H], U8, name="w2_s", align_bytes=64)
         gate_sb = keep.tile([P, TOP, T], F32, name="gate_sb")
         a_sb = keep.tile([P, 4, T], F32, name="a_sb")
-        w1_raw = keep.tile([P, 4, K], F32, name="w1_raw")
+        w1_raw = keep.tile([P, 4, K], F32, name="w1_raw", align_bytes=64)
         w1_w = keep.tile([P, K], U32, name="w1_w", align_bytes=64)
         w1_s = keep.tile([P, K], U8, name="w1_s", align_bytes=64)
         y = [keep.tile([P, S], F32, name=f"y{c}") for c in range(HT)]
@@ -79,12 +79,12 @@ def tile_moe_sub_relu_kernel(
                 )
 
         load_words(0, 3)
-        nc.sync.dma_start(w1_raw[:], w1t.rearrange("(p d) k -> p d k", d=4))
         load_scales(0, 6)
         load_words(3, 6)
         load_scales(6, 16)
         load_words(6, 11)
         load_words(11, 16)
+        nc.sync.dma_start(w1_raw[:], w1t.rearrange("(p d) k -> p d k", d=4))
         for r, pos in enumerate((pos1, pos2, pos3, pos4)):
             nc.sync.dma_start(pos_sb[r][:], pos)
         for r in range(TOP):
@@ -109,12 +109,12 @@ def tile_moe_sub_relu_kernel(
             return later_w[:, (e - FIRST) * C : (e - FIRST + 1) * C]
 
         w1_bf = keep.tile([P, K, 4], BF16, name="w1_bf", align_bytes=64)
-        nc.scalar.copy(w1_bf[:], w1_raw[:].rearrange("p d k -> p k d"))
+        nc.gpsimd.tensor_scalar(w1_bf[:], w1_raw[:].rearrange("p d k -> p k d"), 1.0, 0.0, ALU.mult, ALU.add)
         nc.vector.quantize_mx(
             out=w1_w[:].bitcast(FP8X4), scales=w1_s[:], in_=w1_bf[:].rearrange("p k d -> p (k d)")
         )
 
-        ident = shared.tile([P, P], F32, name="ident", offset=0, align_bytes=64)
+        ident = keep.tile([P, P], F32, name="w1_raw", align_bytes=64)
         nc.gpsimd.affine_select(
             out=ident[:],
             in_=zeros[:],

@@ -23,6 +23,8 @@ TT = T // P
 PIECES = ((0, 3), (3, 6), (6, 9), (9, 12), (12, 15), (15, 16))
 FIRST = PIECES[0][1]
 RING = 6
+PICK_RING = 4
+PRODUCT_RING = 4
 LAST_SPANS = ((0, 2), (2, 3), (3, 4))
 
 
@@ -33,7 +35,6 @@ def tile_moe_sub_relu_kernel(
     with ExitStack() as ctx:
         keep = ctx.enter_context(tc.tile_pool(name="keep", bufs=1))
         shared = ctx.enter_context(tc.tile_pool(name="shared", bufs=1))
-        held = ctx.enter_context(tc.tile_pool(name="held", bufs=1))
         psum = ctx.enter_context(tc.psum_pool(name="psum", bufs=1))
 
         offs_sb = keep.tile([P, S // 16], U16, name="offs_sb")
@@ -81,9 +82,11 @@ def tile_moe_sub_relu_kernel(
         load_words(0, 3)
         load_scales(0, 6)
         load_words(3, 6)
-        load_scales(6, 16)
-        load_words(6, 11)
-        load_words(11, 16)
+        load_scales(6, 12)
+        load_words(6, 9)
+        load_words(9, 12)
+        load_scales(12, 16)
+        load_words(12, 16)
         nc.sync.dma_start(w1_raw[:], w1t.rearrange("(p d) k -> p d k", d=4))
         for r, pos in enumerate((pos1, pos2, pos3, pos4)):
             nc.sync.dma_start(pos_sb[r][:], pos)
@@ -128,8 +131,7 @@ def tile_moe_sub_relu_kernel(
         def take_bank(b):
             return psum.tile([P, 4 * C], F32, name=f"bank{b}")
 
-        def expert_products(c, e0, e1, b):
-            bank = take_bank(b)
+        def expert_products(c, e0, e1, bank):
             for e in range(e0, e1):
                 nc.tensor.matmul_mx(
                     out=bank[:, (e - e0) * C : (e - e0 + 1) * C],
@@ -145,16 +147,15 @@ def tile_moe_sub_relu_kernel(
             else:
                 nc.scalar.activation(y[c][:, e0 * C : e1 * C], bank[:, : (e1 - e0) * C], ACT.Copy)
 
-        steps = [(c, piece) for piece in PIECES[:3] for c in range(HT)]
-        steps.extend(((0, (9, 12)), (1, (9, 12)), (2, (9, 12)), (3, (9, 12)), (0, (12, 15)), (0, (15, 16))))
-        steps.extend((c, (12, 16)) for c in range(1, HT))
+        steps = [(c, piece) for piece in PIECES[:-1] for c in range(HT)]
         for n, (c, (e0, e1)) in enumerate(steps):
-            expert_products(c, e0, e1, n % RING)
+            expert_products(c, e0, e1, take_bank(n % RING))
+        expert_products(0, E - 1, E, take_bank(6))
+        for c in range(1, HT):
+            expert_products(c, E - 1, E, take_bank((7, 2, 3)[c - 1]))
 
-        def place(n, j0, j1, name):
-            return held.tile([P, (j1 - j0) * P], F32, name=name, offset=4 * (n * T + j0 * P))
-
-        def gather_gated(prod, c, r, j0, j1):
+        def gather_gated(c, r, j0, j1):
+            prod = product_tile(j1 - j0)
             nc.vector.tensor_tensor(
                 prod[:],
                 y[c][:].indirect(pos_sb[r][:, j0 * P // 16 : j1 * P // 16]),
@@ -163,31 +164,43 @@ def tile_moe_sub_relu_kernel(
             )
             return prod
 
-        def gather_plain(c, r):
-            picked = place(TOP * c + r, 0, TT, f"picked{c}_{r}")
-            nc.scalar.activation(picked[:], y[c][:].indirect(pos_sb[r][:]), ACT.Copy)
+        picks = []
+        products = []
+
+        def gather_plain(c, r, j0, j1):
+            picked = keep.tile([P, (j1 - j0) * P], F32, name=f"picked{len(picks) % PICK_RING}")
+            picks.append(picked)
+            nc.scalar.activation(
+                picked[:], y[c][:].indirect(pos_sb[r][:, j0 * P // 16 : j1 * P // 16]), ACT.Copy
+            )
             return picked
 
-        def apply_gate(picked, c, r):
-            prod = keep.tile([P, T], F32, name=f"prod{c}_{r}")
-            nc.vector.tensor_tensor(prod[:], picked[:], gate_sb[:, r, :], ALU.mult)
+        def product_tile(width):
+            products.append(keep.tile([P, width * P], F32, name=f"prod{len(products) % PRODUCT_RING}"))
+            return products[-1]
+
+        def apply_gate(picked, r, j0, j1):
+            prod = product_tile(j1 - j0)
+            nc.vector.tensor_tensor(prod[:], picked[:], gate_sb[:, r, j0 * P : j1 * P], ALU.mult)
             return prod
 
-        def add_up(acc, prod, first, j0, j1, start, stop):
-            for j in range(j0, j1):
+        def add_up(places, prod, start, stop):
+            for k, where in enumerate(places):
                 nc.tensor.matmul(
-                    acc[:, (j - j0) * P : (j - j0 + 1) * P],
-                    prod[:, (j - first) * P : (j - first + 1) * P],
+                    where,
+                    prod[:, k * P : (k + 1) * P],
                     ident[:],
-                    start=(start and j == j0),
-                    stop=(stop and j == j1 - 1),
+                    start=start(k),
+                    stop=stop(k),
                     is_transpose=True,
                 )
 
-        def round_sum(acc, c, j0, j1):
+        def round_sum(acc, c0, c1, j0, j1):
             nc.scalar.copy(
-                da_t[:, :, j0:j1, c * P // 2 : (c + 1) * P // 2].rearrange("p u j (q e) -> p u j q e", e=2),
-                acc[:, : (j1 - j0) * P].rearrange("p (j q u e) -> p u j q e", q=32, u=2, e=2),
+                da_t[:, :, j0:j1, c0 * P // 2 : c1 * P // 2].rearrange("p u j (q e) -> p u j q e", e=2),
+                acc[:, : (j1 - j0) * (c1 - c0) * P].rearrange(
+                    "p (j q u e) -> p u j q e", j=j1 - j0, u=2, e=2
+                ),
             )
 
         def turn_back(j):
@@ -237,45 +250,62 @@ def tile_moe_sub_relu_kernel(
                 out.rearrange("(m p) t -> p m t", p=P)[:, :, cols], res[:].rearrange("p (m t) -> p m t", m=2)
             )
 
-        acc = take_bank(RING)
-        picked = gather_plain(0, TOP - 1)
-        for r in range(TOP - 1):
-            add_up(acc, gather_gated(place(r, 0, TT, f"gated0_{r}"), 0, r, 0, TT), 0, 0, TT, r == 0, False)
-        add_up(acc, apply_gate(picked, 0, TOP - 1), 0, 0, TT, False, True)
-        for c in range(1, HT - 1):
-            picked = [gather_plain(c, r) for r in range(1, TOP)]
-            round_sum(acc, c - 1, 0, TT)
-            acc = take_bank((RING + c) % 8)
-            prod = place(TOP * c - 1, 0, TT, f"gated{c}_0")
-            add_up(acc, gather_gated(prod, c, 0, 0, TT), 0, 0, TT, True, False)
-            if c == 1:
-                mask = keep.tile([P, 2, T, 2], BF16, name="y0")
-                nc.vector.tensor_scalar(
-                    mask[:], a_sb[:].rearrange("p (u e) t -> p u t e", u=2), 0.0, None, ALU.is_gt
-                )
-            for r in range(1, TOP):
-                add_up(acc, apply_gate(picked[r - 1], c, r), 0, 0, TT, False, r == TOP - 1)
+        def never(k):
+            return False
 
-        c = HT - 1
-        picked = [gather_plain(c, r) for r in range(2)]
-        round_sum(acc, c - 1, 0, TT)
-        accs = [take_bank(1 + n) for n in range(len(LAST_SPANS))]
-        for r in (2, 3):
-            prod = place(TOP * c - 1, 2 * r - 4, 2 * r - 2, f"gated{c}_{r}_0")
-            add_up(accs[0], gather_gated(prod, c, r, 0, 2), 0, 0, 2, r == 2, False)
-        for r in range(2):
-            prod = apply_gate(picked[r], c, r)
-            for n, (acc, (j0, j1)) in enumerate(zip(accs, LAST_SPANS)):
-                add_up(acc, prod, 0, j0, j1, r == 0 and n > 0, r == 1 and n == 0)
-        turned = []
-        for n, (acc, (j0, j1)) in enumerate(zip(accs, LAST_SPANS)):
-            for r in (2, 3) if n > 0 else ():
-                k = 2 * (n - 1) + r - 2
-                prod = place(TOP * c + 1, k, k + 1, f"gated{c}_{r}_{j0}")
-                add_up(acc, gather_gated(prod, c, r, j0, j1), j0, j0, j1, False, r == TOP - 1)
-            round_sum(acc, c, j0, j1)
-            turned.extend(turn_back(j) for j in range(j0, j1))
+        def first(k):
+            return k == 0
+
+        def always(k):
+            return True
+
+        acc0 = take_bank(6)
+        sums = [acc0[:, j * P : (j + 1) * P] for j in range(TT)]
+        picked = gather_plain(0, 3, 0, TT)
+        for r in range(3):
+            add_up(sums, gather_gated(0, r, 0, TT), first if r == 0 else never, never)
+        add_up(sums, apply_gate(picked, 3, 0, TT), never, lambda k: k == TT - 1)
+
+        acc1 = take_bank(7)
+        sums = [acc1[:, j * P : (j + 1) * P] for j in range(TT)]
+        picked = [gather_plain(1, r, 0, TT) for r in (1, 2, 3)]
+        round_sum(acc0, 0, 1, 0, TT)
+        add_up(sums, gather_gated(1, 0, 0, TT), first, never)
+        mask = keep.tile([P, 2, T, 2], BF16, name="y0")
+        nc.vector.tensor_scalar(mask[:], a_sb[:].rearrange("p (u e) t -> p u t e", u=2), 0.0, None, ALU.is_gt)
+        for r in (1, 2, 3):
+            add_up(sums, apply_gate(picked[r - 1], r, 0, TT), never, lambda k: r == 3 and k == TT - 1)
+
+        acc2 = take_bank(0)
+        sums = [acc2[:, j * P : (j + 1) * P] for j in range(TT)]
+        picked = [gather_plain(2, r, 0, TT) for r in (1, 2, 3)]
+        round_sum(acc1, 1, 2, 0, TT)
+        add_up(sums, gather_gated(2, 0, 0, TT), first, never)
+        for r in (1, 2, 3):
+            add_up(sums, apply_gate(picked[r - 1], r, 0, TT), never, lambda k: r == 3 and k == TT - 1)
+
+        acc3 = take_bank(1)
+        sums = [acc3[:, j * P : (j + 1) * P] for j in range(2)]
+        picked = [gather_plain(3, r, 0, 2) for r in (1, 2, 3)]
+        round_sum(acc2, 2, 3, 0, TT)
+        add_up(sums, gather_gated(3, 0, 0, 2), first, never)
+        for r in (1, 2, 3):
+            add_up(sums, apply_gate(picked[r - 1], r, 0, 2), never, lambda k: r == 3 and k == 1)
+
+        accs = {j: take_bank(j) for j in (2, 3)}
+        sums = [accs[j][:, :P] for j in (2, 3)]
+        round_sum(acc3, 3, 4, 0, 2)
+        turned = [turn_back(0), turn_back(1)]
+        picked = [gather_plain(3, r, 2, 4) for r in (1, 2)]
+        add_up(sums, gather_gated(3, 0, 2, 4), always, never)
+        add_up(sums, apply_gate(picked[0], 1, 2, 4), never, never)
+        add_up(sums[:1], gather_gated(3, 3, 2, 3), never, never)
+        add_up(sums, apply_gate(picked[1], 2, 2, 4), never, first)
+        add_up(sums[1:], gather_gated(3, 3, 3, 4), never, always)
         apply_mask(turned[0], 0)
+        for j in (2, 3):
+            round_sum(accs[j], 3, 4, j, j + 1)
+            turned.append(turn_back(j))
         for j in range(1, TT):
             apply_mask(turned[j], j)
             quantise_da(j - 1)

@@ -82,11 +82,9 @@ def tile_moe_sub_relu_kernel(
         load_words(0, 3)
         load_scales(0, 6)
         load_words(3, 6)
-        load_scales(6, 12)
-        load_words(6, 9)
-        load_words(9, 12)
-        load_scales(12, 16)
-        load_words(12, 16)
+        load_scales(6, 16)
+        load_words(6, 11)
+        load_words(11, 16)
         nc.sync.dma_start(w1_raw[:], w1t.rearrange("(p d) k -> p d k", d=4))
         for r, pos in enumerate((pos1, pos2, pos3, pos4)):
             nc.sync.dma_start(pos_sb[r][:], pos)

@@ -140,7 +140,7 @@ def tile_moe_sub_relu_kernel(
                     start=True,
                     stop=True,
                 )
-            if c == 0 and e0 >= 12:
+            if (c, e0) in ((0, 12), (1, 12), (0, 15)):
                 nc.vector.tensor_copy(y[c][:, e0 * C : e1 * C], bank[:, : (e1 - e0) * C])
             else:
                 nc.scalar.activation(y[c][:, e0 * C : e1 * C], bank[:, : (e1 - e0) * C], ACT.Copy)
@@ -283,23 +283,21 @@ def tile_moe_sub_relu_kernel(
             add_up(sums, apply_gate(picked[r - 1], r, 0, TT), never, lambda k: r == 3 and k == TT - 1)
 
         acc3 = take_bank(1)
-        sums = [acc3[:, j * P : (j + 1) * P] for j in range(2)]
-        picked = [gather_plain(3, r, 0, 2) for r in (1, 2, 3)]
-        round_sum(acc2, 2, 3, 0, TT)
-        add_up(sums, gather_gated(3, 0, 0, 2), first, never)
-        for r in (1, 2, 3):
-            add_up(sums, apply_gate(picked[r - 1], r, 0, 2), never, lambda k: r == 3 and k == 1)
-
         accs = {j: take_bank(j) for j in (2, 3)}
-        sums = [accs[j][:, :P] for j in (2, 3)]
+        sums = [acc3[:, :P], acc3[:, P : 2 * P], accs[2][:, :P], accs[3][:, :P]]
+        whole = gather_plain(3, 1, 0, TT)
+        early = gather_plain(3, 2, 0, 2)
+        round_sum(acc2, 2, 3, 0, TT)
+        late = gather_plain(3, 2, 2, 4)
+        add_up(sums, gather_gated(3, 0, 0, TT), lambda k: k != 1, never)
+        add_up(sums[:2], gather_gated(3, 3, 0, 2), never, never)
+        add_up(sums, apply_gate(whole, 1, 0, TT), never, never)
+        add_up(sums[:2], apply_gate(early, 2, 0, 2), never, lambda k: k == 1)
         round_sum(acc3, 3, 4, 0, 2)
         turned = [turn_back(0), turn_back(1)]
-        picked = [gather_plain(3, r, 2, 4) for r in (1, 2)]
-        add_up(sums, gather_gated(3, 0, 2, 4), always, never)
-        add_up(sums, apply_gate(picked[0], 1, 2, 4), never, never)
-        add_up(sums[:1], gather_gated(3, 3, 2, 3), never, never)
-        add_up(sums, apply_gate(picked[1], 2, 2, 4), never, first)
-        add_up(sums[1:], gather_gated(3, 3, 3, 4), never, always)
+        add_up(sums[2:3], gather_gated(3, 3, 2, 3), never, never)
+        add_up(sums[2:], apply_gate(late, 2, 2, 4), never, first)
+        add_up(sums[3:], gather_gated(3, 3, 3, 4), never, always)
         apply_mask(turned[0], 0)
         for j in (2, 3):
             round_sum(accs[j], 3, 4, j, j + 1)

@@ -257,51 +257,56 @@ def tile_moe_sub_relu_kernel(
         def always(k):
             return True
 
-        acc0 = take_bank(6)
-        sums = [acc0[:, j * P : (j + 1) * P] for j in range(TT)]
-        picked = gather_plain(0, 3, 0, TT)
-        for r in range(3):
-            add_up(sums, gather_gated(0, r, 0, TT), first if r == 0 else never, never)
-        add_up(sums, apply_gate(picked, 3, 0, TT), never, lambda k: k == TT - 1)
+        def last(k):
+            return k == TT - 1
 
-        acc1 = take_bank(7)
-        sums = [acc1[:, j * P : (j + 1) * P] for j in range(TT)]
-        picked = [gather_plain(1, r, 0, TT) for r in (1, 2, 3)]
+        def columns(acc):
+            return [acc[:, j * P : (j + 1) * P] for j in range(TT)]
+
+        acc0, acc1, acc2, acc3 = take_bank(6), take_bank(7), take_bank(0), take_bank(1)
+        accs = {j: take_bank(j) for j in (2, 3)}
+        sums = [columns(acc0), columns(acc1), columns(acc2), columns(acc3)[:2] + [accs[j][:, :P] for j in (2, 3)]]
+
+        picked02 = gather_plain(0, 2, 0, TT)
+        picked03 = gather_plain(0, 3, 0, TT)
+        picked11 = gather_plain(1, 1, 0, TT)
+        picked12 = gather_plain(1, 2, 0, TT)
+        add_up(sums[0], gather_gated(0, 0, 0, TT), first, never)
+        add_up(sums[0], gather_gated(0, 1, 0, TT), never, never)
+        add_up(sums[1], gather_gated(1, 0, 0, TT), first, never)
+        add_up(sums[0], apply_gate(picked02, 2, 0, TT), never, never)
+        picked13 = gather_plain(1, 3, 0, TT)
+        add_up(sums[0], apply_gate(picked03, 3, 0, TT), never, last)
         round_sum(acc0, 0, 1, 0, TT)
-        add_up(sums, gather_gated(1, 0, 0, TT), first, never)
+        picked22 = gather_plain(2, 2, 0, TT)
+        add_up(sums[2], gather_gated(2, 0, 0, TT), first, never)
+        add_up(sums[1], apply_gate(picked11, 1, 0, TT), never, never)
+        picked23 = gather_plain(2, 3, 0, TT)
+        add_up(sums[1], apply_gate(picked12, 2, 0, TT), never, never)
         mask = keep.tile([P, 2, T, 2], BF16, name="y0")
         nc.vector.tensor_scalar(mask[:], a_sb[:].rearrange("p (u e) t -> p u t e", u=2), 0.0, None, ALU.is_gt)
-        for r in (1, 2, 3):
-            add_up(sums, apply_gate(picked[r - 1], r, 0, TT), never, lambda k: r == 3 and k == TT - 1)
-
-        acc2 = take_bank(0)
-        sums = [acc2[:, j * P : (j + 1) * P] for j in range(TT)]
-        picked = [gather_plain(2, r, 0, TT) for r in (1, 2, 3)]
+        add_up(sums[1], apply_gate(picked13, 3, 0, TT), never, last)
         round_sum(acc1, 1, 2, 0, TT)
-        add_up(sums, gather_gated(2, 0, 0, TT), first, never)
-        for r in (1, 2, 3):
-            add_up(sums, apply_gate(picked[r - 1], r, 0, TT), never, lambda k: r == 3 and k == TT - 1)
-
-        acc3 = take_bank(1)
-        accs = {j: take_bank(j) for j in (2, 3)}
-        sums = [acc3[:, :P], acc3[:, P : 2 * P], accs[2][:, :P], accs[3][:, :P]]
-        whole = gather_plain(3, 1, 0, TT)
+        picked31 = gather_plain(3, 1, 0, TT)
+        add_up(sums[2], apply_gate(picked22, 2, 0, TT), never, never)
         early = gather_plain(3, 2, 0, 2)
+        add_up(sums[2], gather_gated(2, 1, 0, TT), never, never)
+        add_up(sums[2], apply_gate(picked23, 3, 0, TT), never, last)
         round_sum(acc2, 2, 3, 0, TT)
         late = gather_plain(3, 2, 2, 4)
-        add_up(sums, gather_gated(3, 0, 0, TT), lambda k: k != 1, never)
-        add_up(sums[:2], gather_gated(3, 3, 0, 2), never, never)
-        add_up(sums, apply_gate(whole, 1, 0, TT), never, never)
-        add_up(sums[:2], apply_gate(early, 2, 0, 2), never, lambda k: k == 1)
+        add_up(sums[3], gather_gated(3, 0, 0, TT), lambda k: k != 1, never)
+        add_up(sums[3], apply_gate(picked31, 1, 0, TT), never, never)
+        add_up(sums[3][:2], gather_gated(3, 3, 0, 2), never, never)
+        add_up(sums[3][:2], apply_gate(early, 2, 0, 2), never, lambda k: k == 1)
         round_sum(acc3, 3, 4, 0, 2)
         turned = [turn_back(0), turn_back(1)]
-        add_up(sums[2:3], gather_gated(3, 3, 2, 3), never, never)
-        add_up(sums[2:], apply_gate(late, 2, 2, 4), never, first)
-        add_up(sums[3:], gather_gated(3, 3, 3, 4), never, always)
-        apply_mask(turned[0], 0)
+        add_up(sums[3][2:3], gather_gated(3, 3, 2, 3), never, never)
+        add_up(sums[3][2:], apply_gate(late, 2, 2, 4), never, first)
+        add_up(sums[3][3:], gather_gated(3, 3, 3, 4), never, always)
         for j in (2, 3):
             round_sum(accs[j], 3, 4, j, j + 1)
             turned.append(turn_back(j))
+        apply_mask(turned[0], 0)
         for j in range(1, TT):
             apply_mask(turned[j], j)
             quantise_da(j - 1)

@@ -49,7 +49,6 @@ def tile_moe_sub_relu_kernel(
         gate_sb = keep.tile([P, TOP, T], F32, name="gate_sb")
         a_sb = keep.tile([P, 4, T], F32, name="a_sb")
         w1_raw = keep.tile([P, 4, K], F32, name="w1_raw", align_bytes=64)
-        w1_w = keep.tile([P, K], U32, name="w1_w", align_bytes=64)
         w1_s = keep.tile([P, K], U8, name="w1_s", align_bytes=64)
         y = [keep.tile([P, S], F32, name=f"y{c}") for c in range(HT)]
         da_t = keep.tile([P, 2, TT, H // 2], BF16, name="da_t", align_bytes=64)
@@ -111,11 +110,8 @@ def tile_moe_sub_relu_kernel(
 
         w1_bf = keep.tile([P, K, 4], BF16, name="w1_bf", align_bytes=64)
         nc.gpsimd.tensor_scalar(w1_bf[:], w1_raw[:].rearrange("p d k -> p k d"), 1.0, 0.0, ALU.mult, ALU.add)
-        nc.vector.quantize_mx(
-            out=w1_w[:].bitcast(FP8X4), scales=w1_s[:], in_=w1_bf[:].rearrange("p k d -> p (k d)")
-        )
 
-        ident = keep.tile([P, P], F32, name="w1_raw", align_bytes=64)
+        ident = keep.tile([P, P], F32, name="ident", align_bytes=64)
         nc.gpsimd.affine_select(
             out=ident[:],
             in_=zeros[:],
@@ -286,6 +282,10 @@ def tile_moe_sub_relu_kernel(
         mask = keep.tile([P, 2, T, 2], BF16, name="y0")
         nc.vector.tensor_scalar(mask[:], a_sb[:].rearrange("p (u e) t -> p u t e", u=2), 0.0, None, ALU.is_gt)
         add_up(sums[1], apply_gate(picked13, 3, 0, TT), never, last)
+        w1_w = shared.tile([P, K], U32, name="w1_w", offset=T, align_bytes=64)
+        nc.vector.quantize_mx(
+            out=w1_w[:].bitcast(FP8X4), scales=w1_s[:], in_=w1_bf[:].rearrange("p k d -> p (k d)")
+        )
         round_sum(acc1, 1, 2, 0, TT)
         picked31 = gather_plain(3, 1, 0, TT)
         add_up(sums[2], apply_gate(picked22, 2, 0, TT), never, never)

@@ -207,7 +207,7 @@ def tile_moe_sub_relu_kernel(
             nc.vector.tensor_tensor(
                 da_bf[:, j * P : (j + 1) * P, :].rearrange("p t (u e) -> p t u e", u=2),
                 turned[:, : 2 * P].bitcast(BF16).rearrange("p (u t e) -> p t u e", u=2, e=2),
-                mask[:, :, j * P : (j + 1) * P, :].rearrange("p u t e -> p t u e"),
+                gates_of_relu[j].rearrange("p u t e -> p t u e"),
                 ALU.mult,
             )
 
@@ -244,6 +244,17 @@ def tile_moe_sub_relu_kernel(
                 out.rearrange("(m p) t -> p m t", p=P)[:, :, cols], res[:].rearrange("p (m t) -> p m t", m=2)
             )
 
+        def make_mask(j0, j1, name):
+            mask = keep.tile([P, 2, (j1 - j0) * P, 2], BF16, name=name)
+            nc.vector.tensor_scalar(
+                mask[:],
+                a_sb[:, :, j0 * P : j1 * P].rearrange("p (u e) t -> p u t e", u=2),
+                0.0,
+                None,
+                ALU.is_gt,
+            )
+            return mask
+
         def never(k):
             return False
 
@@ -279,8 +290,8 @@ def tile_moe_sub_relu_kernel(
         add_up(sums[1], apply_gate(picked11, 1, 0, TT), never, never)
         picked23 = gather_plain(2, 3, 0, TT)
         add_up(sums[1], apply_gate(picked12, 2, 0, TT), never, never)
-        mask = keep.tile([P, 2, T, 2], BF16, name="y0")
-        nc.vector.tensor_scalar(mask[:], a_sb[:].rearrange("p (u e) t -> p u t e", u=2), 0.0, None, ALU.is_gt)
+        early_mask = make_mask(0, 2, "y0")
+        gates_of_relu = [early_mask[:, :, j * P : (j + 1) * P, :] for j in range(2)]
         add_up(sums[1], apply_gate(picked13, 3, 0, TT), never, last)
         w1_w = shared.tile([P, K], U32, name="w1_w", offset=T, align_bytes=64)
         nc.vector.quantize_mx(
@@ -306,6 +317,8 @@ def tile_moe_sub_relu_kernel(
         for j in (2, 3):
             round_sum(accs[j], 3, 4, j, j + 1)
             turned.append(turn_back(j))
+        late_mask = make_mask(2, TT, "y3")
+        gates_of_relu.extend(late_mask[:, :, j * P : (j + 1) * P, :] for j in range(2))
         apply_mask(turned[0], 0)
         for j in range(1, TT):
             apply_mask(turned[j], j)

@@ -22,7 +22,7 @@ HT = H // P
 TT = T // P
 PIECES = ((0, 3), (3, 6), (6, 9), (9, 12), (12, 15), (15, 16))
 FIRST = PIECES[0][1]
-RING = 6
+RING = 8
 PICK_RING = 4
 PRODUCT_RING = 4
 LAST_SPANS = ((0, 2), (2, 3), (3, 4))
@@ -141,12 +141,9 @@ def tile_moe_sub_relu_kernel(
             else:
                 nc.scalar.activation(y[c][:, e0 * C : e1 * C], bank[:, : (e1 - e0) * C], ACT.Copy)
 
-        steps = [(c, piece) for piece in PIECES[:-1] for c in range(HT)]
+        steps = [(c, piece) for piece in PIECES for c in range(HT)]
         for n, (c, (e0, e1)) in enumerate(steps):
             expert_products(c, e0, e1, take_bank(n % RING))
-        expert_products(0, E - 1, E, take_bank(6))
-        for c in range(1, HT):
-            expert_products(c, E - 1, E, take_bank((7, 2, 3)[c - 1]))
 
         def gather_gated(c, r, j0, j1):
             prod = product_tile(j1 - j0)

@@ -23,9 +23,8 @@ TT = T // P
 PIECES = ((0, 3), (3, 6), (6, 9), (9, 12), (12, 15), (15, 16))
 FIRST = PIECES[0][1]
 RING = 8
-PICK_RING = 4
-PRODUCT_RING = 4
-LAST_SPANS = ((0, 2), (2, 3), (3, 4))
+ROW_STEP = 13
+CHOICE_STEP = 40
 
 
 def tile_moe_sub_relu_kernel(
@@ -47,11 +46,13 @@ def tile_moe_sub_relu_kernel(
         w2_w = keep.tile([P, E, 2 * H], U8, name="w2_w", align_bytes=64)
         w2_s = keep.tile([P, E, H], U8, name="w2_s", align_bytes=64)
         gate_sb = keep.tile([P, TOP, T], F32, name="gate_sb")
+        gate_rows = keep.tile([P, P], F32, name="gate_rows")
+        gate_col = keep.tile([P, TOP, TT], F32, name="gate_col")
         a_sb = keep.tile([P, 4, T], F32, name="a_sb")
         w1_raw = keep.tile([P, 4, K], F32, name="w1_raw", align_bytes=64)
         w1_s = keep.tile([P, K], U8, name="w1_s", align_bytes=64)
         y = [keep.tile([P, S], F32, name=f"y{c}") for c in range(HT)]
-        da_t = keep.tile([P, 2, TT, H // 2], BF16, name="da_t", align_bytes=64)
+        da_t = [keep.tile([P, 2, 2, H // 2], BF16, name=f"da_t{h}", align_bytes=64) for h in range(2)]
         da_bf = keep.tile([P, T, 4], BF16, name="da_bf", align_bytes=64)
         da_w = keep.tile([P, T], U32, name="da_w", align_bytes=64)
         da_s = keep.tile([P, T], U8, name="da_s", align_bytes=64)
@@ -85,10 +86,16 @@ def tile_moe_sub_relu_kernel(
         load_words(6, 11)
         load_words(11, 16)
         nc.sync.dma_start(w1_raw[:], w1t.rearrange("(p d) k -> p d k", d=4))
-        for r, pos in enumerate((pos1, pos2, pos3, pos4)):
-            nc.sync.dma_start(pos_sb[r][:], pos)
-        for r in range(TOP):
-            nc.sync.dma_start(gate_sb[:, r, :], gate[r])
+        nc.sync.dma_start(gate_sb[:, 0, :], gate[0])
+        nc.sync.dma_start(pos_sb[0][:], pos1)
+        nc.sync.dma_start(
+            gate_rows[:], gate.rearrange("r q (j p) -> (r q j) p", p=P)[0 : ROW_STEP * P : ROW_STEP, :]
+        )
+        nc.sync.dma_start(gate_sb[:, 1, :], gate[1])
+        nc.sync.dma_start(pos_sb[1][:], pos2)
+        nc.sync.dma_start(gate_sb[:, 2:, :], gate[2:].rearrange("r p t -> p r t"))
+        nc.sync.dma_start(pos_sb[2][:], pos3)
+        nc.sync.dma_start(pos_sb[3][:], pos4)
         nc.sync.dma_start(a_sb[:], a.rearrange("(p d) t -> p d t", d=4))
 
         entries = offs_sb[:, : FIRST * C // 16]
@@ -145,8 +152,8 @@ def tile_moe_sub_relu_kernel(
         for n, (c, (e0, e1)) in enumerate(steps):
             expert_products(c, e0, e1, take_bank(n % RING))
 
-        def gather_gated(c, r, j0, j1):
-            prod = product_tile(j1 - j0)
+        def gather_gated(c, r, j0, j1, place):
+            prod = keep.tile([P, (j1 - j0) * P], F32, name=f"work_{place}")
             nc.vector.tensor_tensor(
                 prod[:],
                 y[c][:].indirect(pos_sb[r][:, j0 * P // 16 : j1 * P // 16]),
@@ -155,25 +162,43 @@ def tile_moe_sub_relu_kernel(
             )
             return prod
 
-        picks = []
-        products = []
-
-        def gather_plain(c, r, j0, j1):
-            picked = keep.tile([P, (j1 - j0) * P], F32, name=f"picked{len(picks) % PICK_RING}")
-            picks.append(picked)
+        def gather_plain(c, r, j0, j1, place):
+            picked = keep.tile([P, (j1 - j0) * P], F32, name=f"work_{place}")
             nc.scalar.activation(
                 picked[:], y[c][:].indirect(pos_sb[r][:, j0 * P // 16 : j1 * P // 16]), ACT.Copy
             )
             return picked
 
-        def product_tile(width):
-            products.append(keep.tile([P, width * P], F32, name=f"prod{len(products) % PRODUCT_RING}"))
-            return products[-1]
+        def turn_plain(picked, c, j0, j1, banks):
+            for j in range(j0, j1):
+                place = banks[j // 2][:, j % 2 * 2 * P : (j % 2 + 1) * 2 * P]
+                nc.tensor.transpose(
+                    place.rearrange("p (u c q e) -> p c q u e", u=2, c=2, e=2)[:, c - 2],
+                    picked[:, (j - j0) * P : (j - j0 + 1) * P],
+                    ident[:],
+                )
 
-        def apply_gate(picked, r, j0, j1):
-            prod = product_tile(j1 - j0)
-            nc.vector.tensor_tensor(prod[:], picked[:], gate_sb[:, r, j0 * P : j1 * P], ALU.mult)
-            return prod
+        partial = {}
+
+        def gate_and_add(r, j, banks):
+            turned_choice = banks[j // 2][:, j % 2 * 2 * P : (j % 2 + 1) * 2 * P]
+            weight = gate_col[:, r, j : j + 1]
+            if r == TOP - 1:
+                nc.vector.scalar_tensor_tensor(
+                    da_t[j // 2][:, :, j % 2, P:],
+                    turned_choice.rearrange("p (u x) -> p u x", u=2),
+                    weight,
+                    partial[j].rearrange("p (u x) -> p u x", u=2),
+                    ALU.mult,
+                    ALU.add,
+                )
+                return
+            total = keep.tile([P, 2 * P], F32, name=f"partial{r % 2}{j}")[:]
+            if r == 0:
+                nc.scalar.activation(total, turned_choice, ACT.Copy, scale=weight)
+            else:
+                nc.vector.scalar_tensor_tensor(total, turned_choice, weight, partial[j], ALU.mult, ALU.add)
+            partial[j] = total
 
         def add_up(places, prod, start, stop):
             for k, where in enumerate(places):
@@ -186,18 +211,16 @@ def tile_moe_sub_relu_kernel(
                     is_transpose=True,
                 )
 
-        def round_sum(acc, c0, c1, j0, j1):
+        def round_sum(acc, c, h):
             nc.scalar.copy(
-                da_t[:, :, j0:j1, c0 * P // 2 : c1 * P // 2].rearrange("p u j (q e) -> p u j q e", e=2),
-                acc[:, : (j1 - j0) * (c1 - c0) * P].rearrange(
-                    "p (j q u e) -> p u j q e", j=j1 - j0, u=2, e=2
-                ),
+                da_t[h][:, :, :, c * P // 2 : (c + 1) * P // 2].rearrange("p u j (q e) -> p u j q e", e=2),
+                acc[:, h * 2 * P : (h + 1) * 2 * P].rearrange("p (j q u e) -> p u j q e", j=2, u=2, e=2),
             )
 
         def turn_back(j):
-            turned = take_bank(TT + j)
+            turned = take_bank((0, 4, 5, 1)[j])
             for u in range(2):
-                nc.tensor.transpose(turned[:, u * P : (u + 1) * P], da_t[:, u, j, :].bitcast(F32), ident[:])
+                nc.tensor.transpose(turned[:, u * P : (u + 1) * P], da_t[j // 2][:, u, j % 2, :].bitcast(F32), ident[:])
             return turned
 
         def apply_mask(turned, j):
@@ -219,8 +242,8 @@ def tile_moe_sub_relu_kernel(
         def project(j):
             cols = slice(j * P, (j + 1) * P)
             last = j == TT - 1
-            result = take_bank(j)
-            halves = [result[:, :P], take_bank(TT)[:, :P] if last else result[:, P : 2 * P]]
+            result = take_bank((6, 2, 3, 7)[j])
+            halves = [result[:, :P], take_bank(0)[:, :P] if last else result[:, P : 2 * P]]
             for m in range(K // P):
                 nc.tensor.matmul_mx(
                     out=halves[m],
@@ -258,61 +281,59 @@ def tile_moe_sub_relu_kernel(
         def first(k):
             return k == 0
 
-        def always(k):
-            return True
-
         def last(k):
             return k == TT - 1
 
         def columns(acc):
             return [acc[:, j * P : (j + 1) * P] for j in range(TT)]
 
-        acc0, acc1, acc2, acc3 = take_bank(6), take_bank(7), take_bank(0), take_bank(1)
-        accs = {j: take_bank(j) for j in (2, 3)}
-        sums = [columns(acc0), columns(acc1), columns(acc2), columns(acc3)[:2] + [accs[j][:, :P] for j in (2, 3)]]
-
-        picked02 = gather_plain(0, 2, 0, TT)
-        picked03 = gather_plain(0, 3, 0, TT)
-        picked11 = gather_plain(1, 1, 0, TT)
-        picked12 = gather_plain(1, 2, 0, TT)
-        add_up(sums[0], gather_gated(0, 0, 0, TT), first, never)
-        add_up(sums[0], gather_gated(0, 1, 0, TT), never, never)
-        add_up(sums[1], gather_gated(1, 0, 0, TT), first, never)
-        add_up(sums[0], apply_gate(picked02, 2, 0, TT), never, never)
-        picked13 = gather_plain(1, 3, 0, TT)
-        add_up(sums[0], apply_gate(picked03, 3, 0, TT), never, last)
-        round_sum(acc0, 0, 1, 0, TT)
-        picked22 = gather_plain(2, 2, 0, TT)
-        add_up(sums[2], gather_gated(2, 0, 0, TT), first, never)
-        add_up(sums[1], apply_gate(picked11, 1, 0, TT), never, never)
-        picked23 = gather_plain(2, 3, 0, TT)
-        add_up(sums[1], apply_gate(picked12, 2, 0, TT), never, never)
-        early_mask = make_mask(0, 2, "y0")
-        gates_of_relu = [early_mask[:, :, j * P : (j + 1) * P, :] for j in range(2)]
-        add_up(sums[1], apply_gate(picked13, 3, 0, TT), never, last)
+        gate_bank = take_bank(2)
+        nc.tensor.transpose(gate_bank[:, :P], gate_rows[:], ident[:])
+        nc.scalar.copy(
+            gate_col[:], gate_bank[:, : TOP * CHOICE_STEP].rearrange("p (r x) -> p r x", r=TOP)[:, :, :TT]
+        )
+        acc0, acc1 = take_bank(0), take_bank(1)
         w1_w = shared.tile([P, K], U32, name="w1_w", offset=T, align_bytes=64)
         nc.vector.quantize_mx(
             out=w1_w[:].bitcast(FP8X4), scales=w1_s[:], in_=w1_bf[:].rearrange("p k d -> p (k d)")
         )
-        round_sum(acc1, 1, 2, 0, TT)
-        picked31 = gather_plain(3, 1, 0, TT)
-        add_up(sums[2], apply_gate(picked22, 2, 0, TT), never, never)
-        early = gather_plain(3, 2, 0, 2)
-        add_up(sums[2], gather_gated(2, 1, 0, TT), never, never)
-        add_up(sums[2], apply_gate(picked23, 3, 0, TT), never, last)
-        round_sum(acc2, 2, 3, 0, TT)
-        late = gather_plain(3, 2, 2, 4)
-        add_up(sums[3], gather_gated(3, 0, 0, TT), lambda k: k != 1, never)
-        add_up(sums[3], apply_gate(picked31, 1, 0, TT), never, never)
-        add_up(sums[3][:2], gather_gated(3, 3, 0, 2), never, never)
-        add_up(sums[3][:2], apply_gate(early, 2, 0, 2), never, lambda k: k == 1)
-        round_sum(acc3, 3, 4, 0, 2)
-        turned = [turn_back(0), turn_back(1)]
-        add_up(sums[3][2:3], gather_gated(3, 3, 2, 3), never, never)
-        add_up(sums[3][2:], apply_gate(late, 2, 2, 4), never, first)
-        add_up(sums[3][3:], gather_gated(3, 3, 3, 4), never, always)
-        for j in (2, 3):
-            round_sum(accs[j], 3, 4, j, j + 1)
+
+        def plain_choice(r, spans, places):
+            banks = [take_bank(4 + 2 * (r % 2) + h) for h in range(2)]
+            for n, (j0, j1) in enumerate(spans):
+                for c in (2, 3):
+                    turn_plain(gather_plain(c, r, j0, j1, places[2 * n + c - 2]), c, j0, j1, banks)
+            return banks
+
+        whole = ((0, TT),)
+        banks0 = plain_choice(0, whole, "ab")
+        add_up(columns(acc0), gather_gated(0, 0, 0, TT, "f"), first, never)
+        add_up(columns(acc1), gather_gated(1, 0, 0, TT, "h"), first, never)
+        banks1 = plain_choice(1, whole, "cd")
+        for j in range(TT):
+            gate_and_add(0, j, banks0)
+        add_up(columns(acc0), gather_gated(0, 1, 0, TT, "i"), never, never)
+        add_up(columns(acc1), gather_gated(1, 1, 0, TT, "a"), never, never)
+        banks2 = plain_choice(2, whole, "eh")
+        add_up(columns(acc0), gather_gated(0, 2, 0, TT, "b"), never, never)
+        add_up(columns(acc0), gather_gated(0, 3, 0, TT, "c"), never, last)
+        for h in range(2):
+            round_sum(acc0, 0, h)
+        add_up(columns(acc1), gather_gated(1, 2, 0, TT, "d"), never, never)
+        add_up(columns(acc1), gather_gated(1, 3, 0, TT, "e"), never, last)
+        early_mask = make_mask(0, 2, "y1")
+        gates_of_relu = [early_mask[:, :, j * P : (j + 1) * P, :] for j in range(2)]
+        for j in range(TT):
+            gate_and_add(1, j, banks1)
+        banks3 = plain_choice(3, ((0, 2), (2, TT)), "fiab")
+        for j in range(TT):
+            gate_and_add(2, j, banks2)
+        turned = []
+        for h in range(2):
+            round_sum(acc1, 1, h)
+            for j in (2 * h, 2 * h + 1):
+                gate_and_add(3, j, banks3)
+        for j in range(TT):
             turned.append(turn_back(j))
         late_mask = make_mask(2, TT, "y3")
         gates_of_relu.extend(late_mask[:, :, j * P : (j + 1) * P, :] for j in range(2))

@@ -173,9 +173,7 @@ def tile_moe_sub_relu_kernel(
             for j in range(j0, j1):
                 place = banks[j // 2][:, j % 2 * 2 * P : (j % 2 + 1) * 2 * P]
                 nc.tensor.transpose(
-                    place.rearrange("p (u c q e) -> p c q u e", u=2, c=2, e=2)[:, c - 2],
-                    picked[:, (j - j0) * P : (j - j0 + 1) * P],
-                    ident[:],
+                    place[:, (c - 2) * P : (c - 1) * P], picked[:, (j - j0) * P : (j - j0 + 1) * P], ident[:]
                 )
 
         partial = {}
@@ -184,14 +182,15 @@ def tile_moe_sub_relu_kernel(
             turned_choice = banks[j // 2][:, j % 2 * 2 * P : (j % 2 + 1) * 2 * P]
             weight = gate_col[:, r, j : j + 1]
             if r == TOP - 1:
-                nc.vector.scalar_tensor_tensor(
-                    da_t[j // 2][:, :, j % 2, P:],
-                    turned_choice.rearrange("p (u x) -> p u x", u=2),
-                    weight,
-                    partial[j].rearrange("p (u x) -> p u x", u=2),
-                    ALU.mult,
-                    ALU.add,
-                )
+                for u in range(2):
+                    nc.vector.scalar_tensor_tensor(
+                        da_t[j // 2][:, u, j % 2, P:].rearrange("p (q e) -> p q e", e=2),
+                        turned_choice.rearrange("p (q u e) -> p u q e", u=2, e=2)[:, u],
+                        weight,
+                        partial[j].rearrange("p (q u e) -> p u q e", u=2, e=2)[:, u],
+                        ALU.mult,
+                        ALU.add,
+                    )
                 return
             total = keep.tile([P, 2 * P], F32, name=f"partial{r % 2}{j}")[:]
             if r == 0:
@@ -307,7 +306,8 @@ def tile_moe_sub_relu_kernel(
 
         whole = ((0, TT),)
         banks0 = plain_choice(0, whole, "ab")
-        add_up(columns(acc0), gather_gated(0, 0, 0, TT, "f"), first, never)
+        add_up(columns(acc0)[:2], gather_gated(0, 0, 0, 2, "f"), first, never)
+        add_up(columns(acc0)[2:], gather_gated(0, 0, 2, TT, "j"), never, never)
         add_up(columns(acc1), gather_gated(1, 0, 0, TT, "h"), first, never)
         banks1 = plain_choice(1, whole, "cd")
         for j in range(TT):
@@ -325,6 +325,7 @@ def tile_moe_sub_relu_kernel(
         gates_of_relu = [early_mask[:, :, j * P : (j + 1) * P, :] for j in range(2)]
         for j in range(TT):
             gate_and_add(1, j, banks1)
+        late_mask = make_mask(2, TT, "y0")
         banks3 = plain_choice(3, ((0, 2), (2, TT)), "fiab")
         for j in range(TT):
             gate_and_add(2, j, banks2)
@@ -335,7 +336,6 @@ def tile_moe_sub_relu_kernel(
                 gate_and_add(3, j, banks3)
         for j in range(TT):
             turned.append(turn_back(j))
-        late_mask = make_mask(2, TT, "y3")
         gates_of_relu.extend(late_mask[:, :, j * P : (j + 1) * P, :] for j in range(2))
         apply_mask(turned[0], 0)
         for j in range(1, TT):

@@ -23,6 +23,8 @@ TT = T // P
 PIECES = ((0, 3), (3, 6), (6, 9), (9, 12), (12, 15), (15, 16))
 FIRST = PIECES[0][1]
 RING = 8
+SMALLEST = 2.0**-126
+STRETCH = 2.0**63
 ROW_STEP = 13
 CHOICE_STEP = 40
 
@@ -177,6 +179,7 @@ def tile_moe_sub_relu_kernel(
                 )
 
         partial = {}
+        totals = {}
 
         def gate_and_add(r, j, banks):
             turned_choice = banks[j // 2][:, j % 2 * 2 * P : (j % 2 + 1) * 2 * P]
@@ -192,7 +195,7 @@ def tile_moe_sub_relu_kernel(
                         ALU.add,
                     )
                 return
-            total = keep.tile([P, 2 * P], F32, name=f"partial{r % 2}{j}")[:]
+            total = totals[r][:, j, :]
             if r == 0:
                 nc.scalar.activation(total, turned_choice, ACT.Copy, scale=weight)
             else:
@@ -263,17 +266,6 @@ def tile_moe_sub_relu_kernel(
                 out.rearrange("(m p) t -> p m t", p=P)[:, :, cols], res[:].rearrange("p (m t) -> p m t", m=2)
             )
 
-        def make_mask(j0, j1, name):
-            mask = keep.tile([P, 2, (j1 - j0) * P, 2], BF16, name=name)
-            nc.vector.tensor_scalar(
-                mask[:],
-                a_sb[:, :, j0 * P : j1 * P].rearrange("p (u e) t -> p u t e", u=2),
-                0.0,
-                None,
-                ALU.is_gt,
-            )
-            return mask
-
         def never(k):
             return False
 
@@ -310,23 +302,43 @@ def tile_moe_sub_relu_kernel(
         add_up(columns(acc0)[2:], gather_gated(0, 0, 2, TT, "j"), never, never)
         add_up(columns(acc1), gather_gated(1, 0, 0, TT, "h"), first, never)
         banks1 = plain_choice(1, whole, "cd")
+        totals[0] = keep.tile([P, TT, 2 * P], F32, name="total0")
         for j in range(TT):
             gate_and_add(0, j, banks0)
         add_up(columns(acc0), gather_gated(0, 1, 0, TT, "i"), never, never)
-        add_up(columns(acc1), gather_gated(1, 1, 0, TT, "a"), never, never)
+        add_up(columns(acc1), gather_gated(1, 1, 0, TT, "m"), never, never)
         banks2 = plain_choice(2, whole, "eh")
-        add_up(columns(acc0), gather_gated(0, 2, 0, TT, "b"), never, never)
-        add_up(columns(acc0), gather_gated(0, 3, 0, TT, "c"), never, last)
+        add_up(columns(acc0), gather_gated(0, 2, 0, TT, "a"), never, never)
+        add_up(columns(acc0), gather_gated(0, 3, 0, TT, "b"), never, last)
         for h in range(2):
             round_sum(acc0, 0, h)
-        add_up(columns(acc1), gather_gated(1, 2, 0, TT, "d"), never, never)
-        add_up(columns(acc1), gather_gated(1, 3, 0, TT, "e"), never, last)
-        early_mask = make_mask(0, 2, "y1")
-        gates_of_relu = [early_mask[:, :, j * P : (j + 1) * P, :] for j in range(2)]
+        add_up(columns(acc1), gather_gated(1, 2, 0, TT, "c"), never, never)
+        last_mask = keep.tile([P, 2, P, 2], BF16, name="y0")
+        nc.vector.tensor_scalar(
+            last_mask[:], a_sb[:, :, 3 * P :].rearrange("p (u e) t -> p u t e", u=2), 0.0, None, ALU.is_gt
+        )
+        add_up(columns(acc1), gather_gated(1, 3, 0, TT, "d"), never, last)
+        clamped = keep.tile([P, 2, 3 * P, 2], BF16, name="gate_sb")
+        gates_of_relu = []
+        for j0, j1 in ((0, 2), (2, 3)):
+            cols = slice(j0 * P, j1 * P)
+            mask = keep.tile([P, 2, (j1 - j0) * P, 2], BF16, name=f"mask{j0}")
+            nc.gpsimd.tensor_scalar(
+                clamped[:, :, cols, :],
+                a_sb[:, :, cols].rearrange("p (u e) t -> p u t e", u=2),
+                SMALLEST,
+                0.0,
+                ALU.min,
+                ALU.max,
+            )
+            nc.gpsimd.tensor_scalar(mask[:], clamped[:, :, cols, :], STRETCH, STRETCH, ALU.mult, ALU.mult)
+            gates_of_relu.extend(mask[:, :, j * P : (j + 1) * P, :] for j in range(j1 - j0))
+        gates_of_relu.append(last_mask[:])
+        totals[1] = keep.tile([P, TT, 2 * P], F32, name="y1")
         for j in range(TT):
             gate_and_add(1, j, banks1)
-        late_mask = make_mask(2, TT, "y0")
-        banks3 = plain_choice(3, ((0, 2), (2, TT)), "fiab")
+        banks3 = plain_choice(3, ((0, 2), (2, TT)), "fima")
+        totals[2] = keep.tile([P, TT, 2 * P], F32, name="total2")
         for j in range(TT):
             gate_and_add(2, j, banks2)
         turned = []
@@ -336,7 +348,6 @@ def tile_moe_sub_relu_kernel(
                 gate_and_add(3, j, banks3)
         for j in range(TT):
             turned.append(turn_back(j))
-        gates_of_relu.extend(late_mask[:, :, j * P : (j + 1) * P, :] for j in range(2))
         apply_mask(turned[0], 0)
         for j in range(1, TT):
             apply_mask(turned[j], j)

@@ -145,7 +145,7 @@ def tile_moe_sub_relu_kernel(
                     start=True,
                     stop=True,
                 )
-            if (c, e0) in ((0, 12), (1, 12), (0, 15)):
+            if (c, e0) in ((0, 12), (1, 12), (0, 15), (1, 15)):
                 nc.vector.tensor_copy(y[c][:, e0 * C : e1 * C], bank[:, : (e1 - e0) * C])
             else:
                 nc.scalar.activation(y[c][:, e0 * C : e1 * C], bank[:, : (e1 - e0) * C], ACT.Copy)
@@ -195,7 +195,7 @@ def tile_moe_sub_relu_kernel(
                         ALU.add,
                     )
                 return
-            total = totals[r][:, j, :]
+            total = totals[r][j // 2][:, j % 2, :]
             if r == 0:
                 nc.scalar.activation(total, turned_choice, ACT.Copy, scale=weight)
             else:
@@ -220,7 +220,7 @@ def tile_moe_sub_relu_kernel(
             )
 
         def turn_back(j):
-            turned = take_bank((0, 4, 5, 1)[j])
+            turned = take_bank((0, 6, 7, 1)[j])
             for u in range(2):
                 nc.tensor.transpose(turned[:, u * P : (u + 1) * P], da_t[j // 2][:, u, j % 2, :].bitcast(F32), ident[:])
             return turned
@@ -243,9 +243,9 @@ def tile_moe_sub_relu_kernel(
 
         def project(j):
             cols = slice(j * P, (j + 1) * P)
-            last = j == TT - 1
-            result = take_bank((6, 2, 3, 7)[j])
-            halves = [result[:, :P], take_bank(0)[:, :P] if last else result[:, P : 2 * P]]
+            last = j >= TT - 2
+            result = take_bank((2, 3, 4, 5)[j])
+            halves = [result[:, :P], take_bank((0, 6)[j - 2])[:, :P] if last else result[:, P : 2 * P]]
             for m in range(K // P):
                 nc.tensor.matmul_mx(
                     out=halves[m],
@@ -258,8 +258,8 @@ def tile_moe_sub_relu_kernel(
                 )
             res = keep.tile([P, 2 * P], F32, name=f"res{j}")
             if last:
-                for m in range(K // P):
-                    nc.vector.tensor_copy(res[:, m * P : (m + 1) * P], halves[m])
+                nc.scalar.copy(res[:, :P], halves[0])
+                nc.vector.tensor_copy(res[:, P:], halves[1])
             else:
                 nc.scalar.copy(res[:], result[:, : 2 * P])
             nc.sync.dma_start(
@@ -290,7 +290,7 @@ def tile_moe_sub_relu_kernel(
         )
 
         def plain_choice(r, spans, places):
-            banks = [take_bank(4 + 2 * (r % 2) + h) for h in range(2)]
+            banks = [take_bank((4, 6, 2, 4)[r] + h) for h in range(2)]
             for n, (j0, j1) in enumerate(spans):
                 for c in (2, 3):
                     turn_plain(gather_plain(c, r, j0, j1, places[2 * n + c - 2]), c, j0, j1, banks)
@@ -302,7 +302,7 @@ def tile_moe_sub_relu_kernel(
         add_up(columns(acc0)[2:], gather_gated(0, 0, 2, TT, "j"), never, never)
         add_up(columns(acc1), gather_gated(1, 0, 0, TT, "h"), first, never)
         banks1 = plain_choice(1, whole, "cd")
-        totals[0] = keep.tile([P, TT, 2 * P], F32, name="total0")
+        totals[0] = [keep.tile([P, 2, 2 * P], F32, name=f"total0{h}") for h in range(2)]
         for j in range(TT):
             gate_and_add(0, j, banks0)
         add_up(columns(acc0), gather_gated(0, 1, 0, TT, "i"), never, never)
@@ -313,7 +313,7 @@ def tile_moe_sub_relu_kernel(
         for h in range(2):
             round_sum(acc0, 0, h)
         add_up(columns(acc1), gather_gated(1, 2, 0, TT, "c"), never, never)
-        last_mask = keep.tile([P, 2, P, 2], BF16, name="y0")
+        last_mask = keep.tile([P, 2, P, 2], BF16, name="last_mask")
         nc.vector.tensor_scalar(
             last_mask[:], a_sb[:, :, 3 * P :].rearrange("p (u e) t -> p u t e", u=2), 0.0, None, ALU.is_gt
         )
@@ -334,11 +334,11 @@ def tile_moe_sub_relu_kernel(
             nc.gpsimd.tensor_scalar(mask[:], clamped[:, :, cols, :], STRETCH, STRETCH, ALU.mult, ALU.mult)
             gates_of_relu.extend(mask[:, :, j * P : (j + 1) * P, :] for j in range(j1 - j0))
         gates_of_relu.append(last_mask[:])
-        totals[1] = keep.tile([P, TT, 2 * P], F32, name="y1")
+        totals[1] = [keep.tile([P, 2, 2 * P], F32, name=f"y{h}") for h in range(2)]
         for j in range(TT):
             gate_and_add(1, j, banks1)
         banks3 = plain_choice(3, ((0, 2), (2, TT)), "fima")
-        totals[2] = keep.tile([P, TT, 2 * P], F32, name="total2")
+        totals[2] = [keep.tile([P, 2, 2 * P], F32, name=f"total2{h}") for h in range(2)]
         for j in range(TT):
             gate_and_add(2, j, banks2)
         turned = []

@@ -41,7 +41,7 @@ def tile_moe_sub_relu_kernel(
         offs_sb = keep.tile([P, S // 16], U16, name="offs_sb")
         pos_sb = [keep.tile([P, T // 16], U16, name=f"pos_sb{r}") for r in range(TOP)]
         dy_w = keep.tile([P, T], I32, name="dy_w", align_bytes=64)
-        dy_s0 = shared.tile([P, T], U8, name="dy_s0", offset=T, align_bytes=64)
+        dy_s0 = shared.tile([P, T], U8, name="dy_s0", offset=4 * K, align_bytes=64)
         dy_s = shared.tile([P, T], U8, name="dy_s", offset=0, align_bytes=64)
         first_w = keep.tile([P, FIRST * C], U32, name="first_w", align_bytes=64)
         slot_s = keep.tile([P, S], U8, name="slot_s", align_bytes=64)
@@ -104,7 +104,7 @@ def tile_moe_sub_relu_kernel(
         nc.vector.tensor_copy(first_w[:], dy_w[:].bitcast(U32).indirect(entries))
         nc.vector.tensor_copy(slot_s[:, : FIRST * C], dy_s0[:].indirect(entries))
         nc.vector.tensor_copy(dy_s[:].bitcast(I32), dy_s0[:].bitcast(I32))
-        later_w = shared.tile([P, S - FIRST * C], U32, name="later_w", offset=T, align_bytes=64)
+        later_w = shared.tile([P, S - FIRST * C], U32, name="later_w", offset=4 * K, align_bytes=64)
         for e0, e1 in PIECES[1:]:
             entries = offs_sb[:, e0 * C // 16 : e1 * C // 16]
             nc.vector.tensor_copy(
@@ -145,14 +145,21 @@ def tile_moe_sub_relu_kernel(
                     start=True,
                     stop=True,
                 )
-            if (c, e0) in ((0, 12), (1, 12), (0, 15), (1, 15)):
+            if (c, e0) in ((0, 12), (0, 15)):
                 nc.vector.tensor_copy(y[c][:, e0 * C : e1 * C], bank[:, : (e1 - e0) * C])
             else:
                 nc.scalar.activation(y[c][:, e0 * C : e1 * C], bank[:, : (e1 - e0) * C], ACT.Copy)
 
-        steps = [(c, piece) for piece in PIECES for c in range(HT)]
+        steps = [(c, piece) for piece in PIECES[:-2] for c in range(HT)]
+        steps.extend((c, piece) for piece in PIECES[-2:] for c in range(2))
+        steps.extend((c, (PIECES[-2][0], E)) for c in range(2, HT))
+        w1_w = shared.tile([P, K], U32, name="w1_w", offset=0, align_bytes=64)
         for n, (c, (e0, e1)) in enumerate(steps):
             expert_products(c, e0, e1, take_bank(n % RING))
+            if (c, e0) == (0, PIECES[-2][0]):
+                nc.vector.quantize_mx(
+                    out=w1_w[:].bitcast(FP8X4), scales=w1_s[:], in_=w1_bf[:].rearrange("p k d -> p (k d)")
+                )
 
         def gather_gated(c, r, j0, j1, place):
             prod = keep.tile([P, (j1 - j0) * P], F32, name=f"work_{place}")
@@ -213,14 +220,14 @@ def tile_moe_sub_relu_kernel(
                     is_transpose=True,
                 )
 
-        def round_sum(acc, c, h):
+        def round_sum(h):
             nc.scalar.copy(
-                da_t[h][:, :, :, c * P // 2 : (c + 1) * P // 2].rearrange("p u j (q e) -> p u j q e", e=2),
-                acc[:, h * 2 * P : (h + 1) * 2 * P].rearrange("p (j q u e) -> p u j q e", j=2, u=2, e=2),
+                da_t[h][:, :, :, :P].rearrange("p u j (q e) -> p u j q e", e=2),
+                sums[h][:].rearrange("p (j q u e) -> p u j q e", j=2, u=2, e=2),
             )
 
         def turn_back(j):
-            turned = take_bank((0, 6, 7, 1)[j])
+            turned = take_bank((6, 7, 2, 3)[j])
             for u in range(2):
                 nc.tensor.transpose(turned[:, u * P : (u + 1) * P], da_t[j // 2][:, u, j % 2, :].bitcast(F32), ident[:])
             return turned
@@ -244,8 +251,8 @@ def tile_moe_sub_relu_kernel(
         def project(j):
             cols = slice(j * P, (j + 1) * P)
             last = j >= TT - 2
-            result = take_bank((2, 3, 4, 5)[j])
-            halves = [result[:, :P], take_bank((0, 6)[j - 2])[:, :P] if last else result[:, P : 2 * P]]
+            result = take_bank((0, 1, 4, 5)[j])
+            halves = [result[:, :P], take_bank((6, 7)[j - 2])[:, :P] if last else result[:, P : 2 * P]]
             for m in range(K // P):
                 nc.tensor.matmul_mx(
                     out=halves[m],
@@ -273,21 +280,17 @@ def tile_moe_sub_relu_kernel(
             return k == 0
 
         def last(k):
-            return k == TT - 1
+            return k % 2 == 1
 
-        def columns(acc):
-            return [acc[:, j * P : (j + 1) * P] for j in range(TT)]
+        def columns(c):
+            return [sums[j // 2][:, (j % 2 * 2 + c) * P : (j % 2 * 2 + c + 1) * P] for j in range(TT)]
 
         gate_bank = take_bank(2)
         nc.tensor.transpose(gate_bank[:, :P], gate_rows[:], ident[:])
         nc.scalar.copy(
             gate_col[:], gate_bank[:, : TOP * CHOICE_STEP].rearrange("p (r x) -> p r x", r=TOP)[:, :, :TT]
         )
-        acc0, acc1 = take_bank(0), take_bank(1)
-        w1_w = shared.tile([P, K], U32, name="w1_w", offset=T, align_bytes=64)
-        nc.vector.quantize_mx(
-            out=w1_w[:].bitcast(FP8X4), scales=w1_s[:], in_=w1_bf[:].rearrange("p k d -> p (k d)")
-        )
+        sums = [take_bank(0), take_bank(1)]
 
         def plain_choice(r, spans, places):
             banks = [take_bank((4, 6, 2, 4)[r] + h) for h in range(2)]
@@ -298,26 +301,24 @@ def tile_moe_sub_relu_kernel(
 
         whole = ((0, TT),)
         banks0 = plain_choice(0, whole, "ab")
-        add_up(columns(acc0)[:2], gather_gated(0, 0, 0, 2, "f"), first, never)
-        add_up(columns(acc0)[2:], gather_gated(0, 0, 2, TT, "j"), never, never)
-        add_up(columns(acc1), gather_gated(1, 0, 0, TT, "h"), first, never)
+        add_up(columns(0)[:2], gather_gated(0, 0, 0, 2, "f"), first, never)
+        add_up(columns(0)[2:], gather_gated(0, 0, 2, TT, "j"), first, never)
+        add_up(columns(1), gather_gated(1, 0, 0, TT, "h"), never, never)
         banks1 = plain_choice(1, whole, "cd")
         totals[0] = [keep.tile([P, 2, 2 * P], F32, name=f"total0{h}") for h in range(2)]
         for j in range(TT):
             gate_and_add(0, j, banks0)
-        add_up(columns(acc0), gather_gated(0, 1, 0, TT, "i"), never, never)
-        add_up(columns(acc1), gather_gated(1, 1, 0, TT, "m"), never, never)
+        add_up(columns(0), gather_gated(0, 1, 0, TT, "i"), never, never)
+        add_up(columns(1), gather_gated(1, 1, 0, TT, "m"), never, never)
         banks2 = plain_choice(2, whole, "eh")
-        add_up(columns(acc0), gather_gated(0, 2, 0, TT, "a"), never, never)
-        add_up(columns(acc0), gather_gated(0, 3, 0, TT, "b"), never, last)
-        for h in range(2):
-            round_sum(acc0, 0, h)
-        add_up(columns(acc1), gather_gated(1, 2, 0, TT, "c"), never, never)
+        add_up(columns(0), gather_gated(0, 2, 0, TT, "a"), never, never)
+        add_up(columns(0), gather_gated(0, 3, 0, TT, "b"), never, never)
+        add_up(columns(1), gather_gated(1, 2, 0, TT, "c"), never, never)
         last_mask = keep.tile([P, 2, P, 2], BF16, name="last_mask")
         nc.vector.tensor_scalar(
             last_mask[:], a_sb[:, :, 3 * P :].rearrange("p (u e) t -> p u t e", u=2), 0.0, None, ALU.is_gt
         )
-        add_up(columns(acc1), gather_gated(1, 3, 0, TT, "d"), never, last)
+        add_up(columns(1), gather_gated(1, 3, 0, TT, "d"), never, last)
         clamped = keep.tile([P, 2, 3 * P, 2], BF16, name="gate_sb")
         gates_of_relu = []
         for j0, j1 in ((0, 2), (2, 3)):
@@ -343,7 +344,7 @@ def tile_moe_sub_relu_kernel(
             gate_and_add(2, j, banks2)
         turned = []
         for h in range(2):
-            round_sum(acc1, 1, h)
+            round_sum(h)
             for j in (2 * h, 2 * h + 1):
                 gate_and_add(3, j, banks3)
         for j in range(TT):

@@ -145,7 +145,7 @@ def tile_moe_sub_relu_kernel(
                     start=True,
                     stop=True,
                 )
-            if (c, e0) in ((0, 12), (0, 15)):
+            if (c, e0) in ((0, 12), (0, 15), (1, 15)):
                 nc.vector.tensor_copy(y[c][:, e0 * C : e1 * C], bank[:, : (e1 - e0) * C])
             else:
                 nc.scalar.activation(y[c][:, e0 * C : e1 * C], bank[:, : (e1 - e0) * C], ACT.Copy)

from contextlib import ExitStack

import concourse.mybir as mybir

K, T, E, C, H, N, TOP = 256, 512, 16, 128, 512, 512, 4
FLOPS = 2 * N * H * E * C + 2 * H * K * T

F32 = mybir.dt.float32
BF16 = mybir.dt.bfloat16
I32 = mybir.dt.int32
U32 = mybir.dt.uint32
U16 = mybir.dt.uint16
U8 = mybir.dt.uint8
FP8X4 = mybir.dt.float8_e4m3fn_x4
FP4X4 = mybir.dt.float4_e2m1fn_x4
ALU = mybir.AluOpType
ACT = mybir.ActivationFunctionType

P = 128
S = E * C
HT = H // P
TT = T // P
PIECES = ((0, 3), (3, 6), (6, 9), (9, 12), (12, 15), (15, 16))
FIRST = PIECES[0][1]
RING = 8
SMALLEST = 2.0**-126
STRETCH = 2.0**63
ROW_STEP = 13
CHOICE_STEP = 40


def tile_moe_sub_relu_kernel(
    tc, dy_words, dy_scales, w2t_words, w2t_scales, w1t, a, gate, offs, pos1, pos2, pos3, pos4, out
):
    nc = tc.nc
    with ExitStack() as ctx:
        keep = ctx.enter_context(tc.tile_pool(name="keep", bufs=1))
        shared = ctx.enter_context(tc.tile_pool(name="shared", bufs=1))
        psum = ctx.enter_context(tc.psum_pool(name="psum", bufs=1))

        offs_sb = keep.tile([P, S // 16], U16, name="offs_sb")
        pos_sb = [keep.tile([P, T // 16], U16, name=f"pos_sb{r}") for r in range(TOP)]
        dy_w = keep.tile([P, T], I32, name="dy_w", align_bytes=64)
        dy_s0 = shared.tile([P, T], U8, name="dy_s0", offset=4 * K, align_bytes=64)
        dy_s = shared.tile([P, T], U8, name="dy_s", offset=0, align_bytes=64)
        first_w = keep.tile([P, FIRST * C], U32, name="first_w", align_bytes=64)
        slot_s = keep.tile([P, S], U8, name="slot_s", align_bytes=64)
        w2_w = keep.tile([P, E, 2 * H], U8, name="w2_w", align_bytes=64)
        w2_s = keep.tile([P, E, H], U8, name="w2_s", align_bytes=64)
        gate_sb = keep.tile([P, TOP, T], F32, name="gate_sb")
        gate_rows = keep.tile([P, P], F32, name="gate_rows")
        gate_col = keep.tile([P, TOP, TT], F32, name="gate_col")
        a_sb = keep.tile([P, 4, T], F32, name="a_sb")
        w1_raw = keep.tile([P, 4, K], F32, name="w1_raw", align_bytes=64)
        w1_s = keep.tile([P, K], U8, name="w1_s", align_bytes=64)
        y = [keep.tile([P, S], F32, name=f"y{c}") for c in range(HT)]
        da_t = [keep.tile([P, 2, 2, H // 2], BF16, name=f"da_t{h}", align_bytes=64) for h in range(2)]
        da_bf = keep.tile([P, T, 4], BF16, name="da_bf", align_bytes=64)
        da_w = keep.tile([P, T], U32, name="da_w", align_bytes=64)
        da_s = keep.tile([P, T], U8, name="da_s", align_bytes=64)
        zeros = keep.tile([P, P], F32, name="zeros")

        nc.vector.memset(dy_s0[:].bitcast(I32), 0)
        nc.vector.memset(zeros[:], 0.0)

        nc.sync.dma_start(dy_w[:], dy_words[0].rearrange("p t d -> p (t d)").bitcast(I32))
        nc.sync.dma_start(offs_sb[:], offs)
        for r in range(4):
            nc.sync.dma_start(dy_s0[r:P:32, :].bitcast(I32), dy_scales[0, r:16:4, :].bitcast(I32))

        def load_words(e0, e1):
            nc.sync.dma_start(
                w2_w[:, e0:e1, :].bitcast(I32),
                w2t_words[e0:e1, 0].rearrange("e p b -> p e b").bitcast(I32),
            )

        def load_scales(e0, e1):
            for r in range(4):
                nc.sync.dma_start(
                    w2_s[r:P:32, e0:e1, :].bitcast(I32),
                    w2t_scales[e0:e1, 0, r:16:4, :].rearrange("e q i -> q e i").bitcast(I32),
                )

        load_words(0, 3)
        load_scales(0, 6)
        load_words(3, 6)
        load_scales(6, 16)
        load_words(6, 11)
        load_words(11, 16)
        nc.sync.dma_start(w1_raw[:], w1t.rearrange("(p d) k -> p d k", d=4))
        nc.sync.dma_start(gate_sb[:, 0, :], gate[0])
        nc.sync.dma_start(pos_sb[0][:], pos1)
        nc.sync.dma_start(
            gate_rows[:], gate.rearrange("r q (j p) -> (r q j) p", p=P)[0 : ROW_STEP * P : ROW_STEP, :]
        )
        nc.sync.dma_start(gate_sb[:, 1, :], gate[1])
        nc.sync.dma_start(pos_sb[1][:], pos2)
        nc.sync.dma_start(gate_sb[:, 2:, :], gate[2:].rearrange("r p t -> p r t"))
        nc.sync.dma_start(pos_sb[2][:], pos3)
        nc.sync.dma_start(pos_sb[3][:], pos4)
        nc.sync.dma_start(a_sb[:], a.rearrange("(p d) t -> p d t", d=4))

        entries = offs_sb[:, : FIRST * C // 16]
        nc.vector.tensor_copy(first_w[:], dy_w[:].bitcast(U32).indirect(entries))
        nc.vector.tensor_copy(slot_s[:, : FIRST * C], dy_s0[:].indirect(entries))
        nc.vector.tensor_copy(dy_s[:].bitcast(I32), dy_s0[:].bitcast(I32))
        later_w = shared.tile([P, S - FIRST * C], U32, name="later_w", offset=4 * K, align_bytes=64)
        for e0, e1 in PIECES[1:]:
            entries = offs_sb[:, e0 * C // 16 : e1 * C // 16]
            nc.vector.tensor_copy(
                later_w[:, (e0 - FIRST) * C : (e1 - FIRST) * C], dy_w[:].bitcast(U32).indirect(entries)
            )
            nc.vector.tensor_copy(slot_s[:, e0 * C : e1 * C], dy_s[:].indirect(entries))

        def slot_words(e):
            if e < FIRST:
                return first_w[:, e * C : (e + 1) * C]
            return later_w[:, (e - FIRST) * C : (e - FIRST + 1) * C]

        w1_bf = keep.tile([P, K, 4], BF16, name="w1_bf", align_bytes=64)
        nc.gpsimd.tensor_scalar(w1_bf[:], w1_raw[:].rearrange("p d k -> p k d"), 1.0, 0.0, ALU.mult, ALU.add)

        ident = keep.tile([P, P], F32, name="ident", align_bytes=64)
        nc.gpsimd.affine_select(
            out=ident[:],
            in_=zeros[:],
            compare_op=ALU.not_equal,
            fill=1.0,
            base=0,
            pattern=[[-1, P]],
            channel_multiplier=1,
        )

        def take_bank(b):
            return psum.tile([P, 4 * C], F32, name=f"bank{b}")

        def expert_products(c, e0, e1, bank):
            for e in range(e0, e1):
                nc.tensor.matmul_mx(
                    out=bank[:, (e - e0) * C : (e - e0 + 1) * C],
                    lhsT=w2_w[:, e, 2 * P * c : 2 * P * (c + 1)].bitcast(FP4X4),
                    lhsT_scale=w2_s[:, e, P * c : P * (c + 1)],
                    rhs=slot_words(e).bitcast(FP8X4),
                    rhs_scale=slot_s[:, e * C : (e + 1) * C],
                    start=True,
                    stop=True,
                )
            if (c, e0) in ((0, 12), (0, 15), (1, 15)):
                nc.vector.tensor_copy(y[c][:, e0 * C : e1 * C], bank[:, : (e1 - e0) * C])
            else:
                nc.scalar.activation(y[c][:, e0 * C : e1 * C], bank[:, : (e1 - e0) * C], ACT.Copy)

        steps = [(c, piece) for piece in PIECES[:-2] for c in range(HT)]
        steps.extend((c, piece) for piece in PIECES[-2:] for c in range(2))
        steps.extend((c, (PIECES[-2][0], E)) for c in range(2, HT))
        w1_w = shared.tile([P, K], U32, name="w1_w", offset=0, align_bytes=64)
        for n, (c, (e0, e1)) in enumerate(steps):
            expert_products(c, e0, e1, take_bank(n % RING))
            if (c, e0) == (0, PIECES[-2][0]):
                nc.vector.quantize_mx(
                    out=w1_w[:].bitcast(FP8X4), scales=w1_s[:], in_=w1_bf[:].rearrange("p k d -> p (k d)")
                )

        def gather_gated(c, r, j0, j1, place):
            prod = keep.tile([P, (j1 - j0) * P], F32, name=f"work_{place}")
            nc.vector.tensor_tensor(
                prod[:],
                y[c][:].indirect(pos_sb[r][:, j0 * P // 16 : j1 * P // 16]),
                gate_sb[:, r, j0 * P : j1 * P],
                ALU.mult,
            )
            return prod

        def gather_plain(c, r, j0, j1, place):
            picked = keep.tile([P, (j1 - j0) * P], F32, name=f"work_{place}")
            nc.scalar.activation(
                picked[:], y[c][:].indirect(pos_sb[r][:, j0 * P // 16 : j1 * P // 16]), ACT.Copy
            )
            return picked

        def turn_plain(picked, c, j0, j1, banks):
            for j in range(j0, j1):
                place = banks[j // 2][:, j % 2 * 2 * P : (j % 2 + 1) * 2 * P]
                nc.tensor.transpose(
                    place[:, (c - 2) * P : (c - 1) * P], picked[:, (j - j0) * P : (j - j0 + 1) * P], ident[:]
                )

        partial = {}
        totals = {}

        def gate_and_add(r, j, banks):
            turned_choice = banks[j // 2][:, j % 2 * 2 * P : (j % 2 + 1) * 2 * P]
            weight = gate_col[:, r, j : j + 1]
            if r == TOP - 1:
                for u in range(2):
                    nc.vector.scalar_tensor_tensor(
                        da_t[j // 2][:, u, j % 2, P:].rearrange("p (q e) -> p q e", e=2),
                        turned_choice.rearrange("p (q u e) -> p u q e", u=2, e=2)[:, u],
                        weight,
                        partial[j].rearrange("p (q u e) -> p u q e", u=2, e=2)[:, u],
                        ALU.mult,
                        ALU.add,
                    )
                return
            total = totals[r][j // 2][:, j % 2, :]
            if r == 0:
                nc.scalar.activation(total, turned_choice, ACT.Copy, scale=weight)
            else:
                nc.vector.scalar_tensor_tensor(total, turned_choice, weight, partial[j], ALU.mult, ALU.add)
            partial[j] = total

        def add_up(places, prod, start, stop):
            for k, where in enumerate(places):
                nc.tensor.matmul(
                    where,
                    prod[:, k * P : (k + 1) * P],
                    ident[:],
                    start=start(k),
                    stop=stop(k),
                    is_transpose=True,
                )

        def round_sum(h):
            nc.scalar.copy(
                da_t[h][:, :, :, :P].rearrange("p u j (q e) -> p u j q e", e=2),
                sums[h][:].rearrange("p (j q u e) -> p u j q e", j=2, u=2, e=2),
            )

        def turn_back(j):
            turned = take_bank((6, 7, 2, 3)[j])
            for u in range(2):
                nc.tensor.transpose(turned[:, u * P : (u + 1) * P], da_t[j // 2][:, u, j % 2, :].bitcast(F32), ident[:])
            return turned

        def apply_mask(turned, j):
            nc.vector.tensor_tensor(
                da_bf[:, j * P : (j + 1) * P, :].rearrange("p t (u e) -> p t u e", u=2),
                turned[:, : 2 * P].bitcast(BF16).rearrange("p (u t e) -> p t u e", u=2, e=2),
                gates_of_relu[j].rearrange("p u t e -> p t u e"),
                ALU.mult,
            )

        def quantise_da(j):
            cols = slice(j * P, (j + 1) * P)
            nc.vector.quantize_mx(
                out=da_w[:, cols].bitcast(FP8X4),
                scales=da_s[:, cols],
                in_=da_bf[:, cols, :].rearrange("p t d -> p (t d)"),
            )

        def project(j):
            cols = slice(j * P, (j + 1) * P)
            last = j >= TT - 2
            result = take_bank((0, 1, 4, 5)[j])
            halves = [result[:, :P], take_bank((6, 7)[j - 2])[:, :P] if last else result[:, P : 2 * P]]
            for m in range(K // P):
                nc.tensor.matmul_mx(
                    out=halves[m],
                    lhsT=w1_w[:, m * P : (m + 1) * P].bitcast(FP8X4),
                    lhsT_scale=w1_s[:, m * P : (m + 1) * P],
                    rhs=da_w[:, cols].bitcast(FP8X4),
                    rhs_scale=da_s[:, cols],
                    start=True,
                    stop=True,
                )
            res = keep.tile([P, 2 * P], F32, name=f"res{j}")
            if last:
                nc.scalar.copy(res[:, :P], halves[0])
                nc.vector.tensor_copy(res[:, P:], halves[1])
            else:
                nc.scalar.copy(res[:], result[:, : 2 * P])
            nc.sync.dma_start(
                out.rearrange("(m p) t -> p m t", p=P)[:, :, cols], res[:].rearrange("p (m t) -> p m t", m=2)
            )

        def never(k):
            return False

        def first(k):
            return k == 0

        def last(k):
            return k % 2 == 1

        def columns(c):
            return [sums[j // 2][:, (j % 2 * 2 + c) * P : (j % 2 * 2 + c + 1) * P] for j in range(TT)]

        gate_bank = take_bank(2)
        nc.tensor.transpose(gate_bank[:, :P], gate_rows[:], ident[:])
        nc.scalar.copy(
            gate_col[:], gate_bank[:, : TOP * CHOICE_STEP].rearrange("p (r x) -> p r x", r=TOP)[:, :, :TT]
        )
        sums = [take_bank(0), take_bank(1)]

        def plain_choice(r, spans, places):
            banks = [take_bank((4, 6, 2, 4)[r] + h) for h in range(2)]
            for n, (j0, j1) in enumerate(spans):
                for c in (2, 3):
                    turn_plain(gather_plain(c, r, j0, j1, places[2 * n + c - 2]), c, j0, j1, banks)
            return banks

        whole = ((0, TT),)
        banks0 = plain_choice(0, whole, "ab")
        add_up(columns(0)[:2], gather_gated(0, 0, 0, 2, "f"), first, never)
        add_up(columns(0)[2:], gather_gated(0, 0, 2, TT, "j"), first, never)
        add_up(columns(1), gather_gated(1, 0, 0, TT, "h"), never, never)
        banks1 = plain_choice(1, whole, "cd")
        totals[0] = [keep.tile([P, 2, 2 * P], F32, name=f"total0{h}") for h in range(2)]
        for j in range(TT):
            gate_and_add(0, j, banks0)
        add_up(columns(0), gather_gated(0, 1, 0, TT, "i"), never, never)
        add_up(columns(1), gather_gated(1, 1, 0, TT, "m"), never, never)
        banks2 = plain_choice(2, whole, "eh")
        add_up(columns(0), gather_gated(0, 2, 0, TT, "a"), never, never)
        add_up(columns(0), gather_gated(0, 3, 0, TT, "b"), never, never)
        add_up(columns(1), gather_gated(1, 2, 0, TT, "c"), never, never)
        last_mask = keep.tile([P, 2, P, 2], BF16, name="last_mask")
        nc.vector.tensor_scalar(
            last_mask[:], a_sb[:, :, 3 * P :].rearrange("p (u e) t -> p u t e", u=2), 0.0, None, ALU.is_gt
        )
        add_up(columns(1), gather_gated(1, 3, 0, TT, "d"), never, last)
        clamped = keep.tile([P, 2, 3 * P, 2], BF16, name="gate_sb")
        gates_of_relu = []
        for j0, j1 in ((0, 2), (2, 3)):
            cols = slice(j0 * P, j1 * P)
            mask = keep.tile([P, 2, (j1 - j0) * P, 2], BF16, name=f"mask{j0}")
            nc.gpsimd.tensor_scalar(
                clamped[:, :, cols, :],
                a_sb[:, :, cols].rearrange("p (u e) t -> p u t e", u=2),
                SMALLEST,
                0.0,
                ALU.min,
                ALU.max,
            )
            nc.gpsimd.tensor_scalar(mask[:], clamped[:, :, cols, :], STRETCH, STRETCH, ALU.mult, ALU.mult)
            gates_of_relu.extend(mask[:, :, j * P : (j + 1) * P, :] for j in range(j1 - j0))
        gates_of_relu.append(last_mask[:])
        totals[1] = [keep.tile([P, 2, 2 * P], F32, name=f"y{h}") for h in range(2)]
        for j in range(TT):
            gate_and_add(1, j, banks1)
        banks3 = plain_choice(3, ((0, 2), (2, TT)), "fima")
        totals[2] = [keep.tile([P, 2, 2 * P], F32, name=f"total2{h}") for h in range(2)]
        for j in range(TT):
            gate_and_add(2, j, banks2)
        turned = []
        for h in range(2):
            round_sum(h)
            for j in (2 * h, 2 * h + 1):
                gate_and_add(3, j, banks3)
        for j in range(TT):
            turned.append(turn_back(j))
        apply_mask(turned[0], 0)
        for j in range(1, TT):
            apply_mask(turned[j], j)
            quantise_da(j - 1)
        quantise_da(TT - 1)
        for j in range(TT):
            project(j)
